import numpy as np
import ml_dtypes


def mxq(x, axis, fmt="e4m3"):
    dtype, down = {"e4m3": (ml_dtypes.float8_e4m3fn, 7), "e5m2": (ml_dtypes.float8_e5m2, 14)}[fmt]
    v = np.moveaxis(np.asarray(x, np.float32).astype(ml_dtypes.bfloat16).astype(np.float64), axis, -1)
    blocks = v.reshape(v.shape[:-1] + (-1, 32))
    amax = np.abs(blocks).max(-1, keepdims=True)
    byte = np.maximum(np.where(amax > 0, np.frexp(amax)[1] - 1 + 127, 0) - down, 1)
    scale = np.exp2(byte - 127.0)
    codes = (blocks / scale).astype(np.float32).astype(dtype).astype(np.float64)
    return np.moveaxis((codes * scale).reshape(v.shape), -1, axis)


WIDE = False


def mx_kscale(k):
    if not WIDE:
        return np.ones(k)
    levels = np.array([10, -10, 5, -5, 0])
    if k % 512:
        return np.exp2(np.random.permutation(np.resize(levels, k // 32))).repeat(32)
    a = np.empty((k // 512, 16))
    for p in range(k // 512):
        a[p, :8] = np.random.permutation(np.resize(levels, 8))
        for g in range(8):
            far = levels[np.abs(levels - a[p, g]) >= 10]
            a[p, g + 8] = far[np.random.randint(len(far))]
    return np.exp2(a.ravel()).repeat(32)


BF16 = ml_dtypes.bfloat16


def bf(x):
    return np.asarray(x, np.float32).astype(BF16)


def f64(x):
    return np.asarray(x).astype(np.float64)


T, D = 1024, 1024


def layer_norm(z, gain, shift):
    c = z - z.mean(axis=1, keepdims=True)
    return c / np.sqrt((c * c).mean(axis=1, keepdims=True)) * gain + shift


def draw0():
    s, t = mx_kscale(T), mx_kscale(D)
    return {"x": bf(np.random.standard_normal((T, D)) * s[:, None] * t),
            "a_re": bf(np.random.standard_normal((T, T)) / np.sqrt(T) / s[:, None]),
            "a_im": bf(np.random.standard_normal((T, T)) / np.sqrt(T) / s[:, None]),
            "c_re": bf(np.random.standard_normal((D, T)) * np.sqrt(0.5)),
            "c_im": bf(np.random.standard_normal((D, T)) * np.sqrt(0.5)),
            "w_re": bf(np.random.standard_normal((D, D)) / np.sqrt(2 * D) / t[:, None]),
            "w_im": bf(np.random.standard_normal((D, D)) / np.sqrt(2 * D) / t[:, None]),
            "bias": bf(0.3 * np.random.standard_normal(D)),
            "resid": bf(np.random.standard_normal((T, D))),
            "gain": bf(1 + 0.1 * np.random.standard_normal(D)),
            "shift": bf(0.3 * np.random.standard_normal(D))}


def core(x, a_re, a_im, c_re, c_im, w_re, w_im, bias, resid, gain, shift):
    xq = mxq(f64(x), 0, "e4m3")
    h_re = xq.T @ mxq(f64(a_re), 0, "e4m3")
    h_im = xq.T @ mxq(f64(a_im), 0, "e4m3")
    cr, ci = f64(c_re), f64(c_im)
    g_re = h_re * cr - h_im * ci
    g_im = h_re * ci + h_im * cr
    y_re = mxq(g_re, 0, "e4m3").T @ mxq(f64(w_re), 0, "e4m3")
    y_im = mxq(g_im, 0, "e4m3").T @ mxq(f64(w_im), 0, "e4m3")
    z = f64(resid) + (y_re - y_im) + f64(bias)
    return layer_norm(z, f64(gain), f64(shift))


def e4m3fn_bytes(y):
    return np.clip(np.asarray(y, np.float64), -448.0, 448.0).astype(np.float32).astype(ml_dtypes.float8_e4m3fn).view(np.uint8)


def e4m3fn_values(b):
    return np.asarray(b, np.uint8).view(ml_dtypes.float8_e4m3fn).astype(np.float64)


def setup_inputs():
    d = draw0()
    x0 = np.asarray(d['w_re']).astype(np.float64)
    s = (np.max(np.abs(x0), axis=(1,), keepdims=True) / 448.0).astype(np.float32)
    out = {}
    for k, v in d.items():
        if k == 'w_re':
            out['w_re_bytes'] = e4m3fn_bytes(x0 / s.astype(np.float64))
            out['w_re_scale'] = s
        else:
            out[k] = v
    return out


def reference(x, a_re, a_im, c_re, c_im, w_re_bytes, w_re_scale, w_im, bias, resid, gain, shift):
    return core(x, a_re, a_im, c_re, c_im, e4m3fn_values(w_re_bytes) * w_re_scale.astype(np.float64), w_im, bias, resid, gain, shift)

@@ -1,0 +1,415 @@
+from contextlib import ExitStack
+
+import concourse.mybir as mybir
+from concourse.masks import make_identity
+
+T = 1024
+D = 1024
+FLOPS = 8 * D * T * T
+
+P = 128
+NJ = 4
+HALF = 512
+QUART = 256
+N_GROUPS = 8
+N_FT = 8
+
+F32 = mybir.dt.float32
+BF16 = mybir.dt.bfloat16
+U32 = mybir.dt.uint32
+U8 = mybir.dt.uint8
+FP8 = mybir.dt.float8_e4m3fn
+FP8X4 = mybir.dt.float8_e4m3fn_x4
+ALU = mybir.AluOpType
+ACT = mybir.ActivationFunctionType
+
+GP_TILES = (1, 3, 5)
+
+
+def tile_fourier_token_mixer_f4_kernel(
+    tc, x, a_re, a_im, c_re, c_im, w_re_bytes, w_re_scale, w_im, bias, resid, gain, shift, out
+):
+    nc = tc.nc
+    with ExitStack() as ctx:
+        keep = ctx.enter_context(tc.tile_pool(name="keep", bufs=1))
+        ring = ctx.enter_context(tc.tile_pool(name="ring", bufs=5))
+        cpool = ctx.enter_context(tc.tile_pool(name="cpool", bufs=3))
+        ilpool = ctx.enter_context(tc.tile_pool(name="ilpool", bufs=4))
+        gpool = ctx.enter_context(tc.tile_pool(name="gpool", bufs=2))
+        prod = ctx.enter_context(tc.tile_pool(name="prod", bufs=2))
+        hps = ctx.enter_context(tc.psum_pool(name="hps", bufs=4))
+        yps = ctx.enter_context(tc.psum_pool(name="yps", bufs=4))
+        ctx.enter_context(tc.manual_schedule())
+
+        ident = keep.tile([P, P], BF16, name="ident")
+        ones = keep.tile([P, P], BF16, name="ones")
+        rows = keep.tile([P, 3, D], BF16, name="rows")
+        tiny = keep.tile([P, 1], F32, name="tiny")
+        nc.gpsimd.memset(tiny[:], 1.0)
+        nc.scalar.activation(out=tiny[:], in_=tiny[:], func=ACT.Sqrt)
+        make_identity(nc, ident[:])
+        nc.gpsimd.memset(ones[:], 1.0)
+        nc.gpsimd.memset(rows[:], 0.0)
+
+        xv = x.rearrange("(g p j) d -> p g j d", g=2, j=NJ)
+        av = (a_re.rearrange("(g p j) f -> p g j f", g=2, j=NJ), a_im.rearrange("(g p j) f -> p g j f", g=2, j=NJ))
+        cv = (c_re.rearrange("(q p t) f -> p q t f", q=2, t=NJ), c_im.rearrange("(q p t) f -> p q t f", q=2, t=NJ))
+        wbv = w_re_bytes.rearrange("(q p j) e -> p q j e", q=2, j=NJ)
+        wiv = w_im.rearrange("(q p j) e -> p q j e", q=2, j=NJ)
+        scv = w_re_scale.rearrange("(q p j) o -> p q (j o)", q=2, j=NJ)
+        rv = resid.rearrange("(i p) e -> p i e", p=P)
+
+        def raw_tile(name):
+            return ring.tile([P, 2, NJ, HALF], BF16, tag="raw", name=name, align_bytes=64)
+
+        def load_half(raw, view, h):
+            for g in range(2):
+                nc.sync.dma_start(out=raw[:, g], in_=view[:, g, :, h * HALF : (h + 1) * HALF])
+
+        c_tiles = {}
+
+        def load_c(q, h):
+            ct = cpool.tile([P, 2, NJ, HALF], BF16, tag="c", name="c")
+            for part in range(2):
+                nc.sync.dma_start(out=ct[:, part], in_=cv[part][:, q, :, h * HALF : (h + 1) * HALF])
+            c_tiles[(q, h)] = ct
+
+        x_raw = []
+        a_raw = {}
+        x_raw.append(raw_tile("x0"))
+        load_half(x_raw[0], xv, 0)
+        for part in range(2):
+            a_raw[(part, 0)] = raw_tile("a0")
+            load_half(a_raw[(part, 0)], av[part], 0)
+        load_c(0, 0)
+        x_raw.append(raw_tile("x1"))
+        load_half(x_raw[1], xv, 1)
+        load_c(1, 0)
+
+        wscale = keep.tile([P, 2, NJ], F32, name="wscale")
+        wbytes = keep.tile([P, 2, NJ, D], U8, name="wbytes")
+        res = keep.tile([P, N_FT, D], BF16, name="res")
+        gain_b = keep.tile([P, D], BF16, name="gain_b")
+        shift_b = keep.tile([P, D], BF16, name="shift_b")
+
+        def codes_tile(name, width):
+            return (
+                keep.tile([P, width], U32, name=name + "_c", align_bytes=64),
+                keep.tile([P, width], U8, name=name + "_s", align_bytes=64),
+            )
+
+        xq = {(q, g): codes_tile("xq%d%d" % (q, g), HALF) for q in range(2) for g in range(2)}
+        aq = {
+            (part, h, g): codes_tile("aq%d%d%d" % (part, h, g), HALF)
+            for part in range(2)
+            for h in range(2)
+            for g in range(2)
+        }
+        wq = {
+            (part, q, e): codes_tile("wq%d%d%d" % (part, q, e), HALF)
+            for part in range(2)
+            for q in range(2)
+            for e in range(2)
+        }
+        gq = {
+            (part, fq, q): codes_tile("gq%d%d%d" % (part, fq, q), QUART)
+            for part in range(2)
+            for fq in range(4)
+            for q in range(2)
+        }
+
+        def il_tile():
+            return ilpool.tile([P, NJ * HALF], BF16, tag="il", name="il", align_bytes=64)
+
+        def copy_on(eng, o, i):
+            if eng == "V":
+                nc.vector.tensor_copy(out=o, in_=i)
+            else:
+                nc.scalar.copy(out=o, in_=i)
+
+        def inter_x(eng, q, g):
+            il = il_tile()
+            copy_on(
+                eng,
+                il[:].rearrange("p (t m j) -> p m t j", t=NJ, j=NJ),
+                x_raw[q][:, g].rearrange("p j (m t) -> p m t j", t=NJ),
+            )
+            return il
+
+        def inter(eng, rows4):
+            il = il_tile()
+            copy_on(
+                eng,
+                il[:].rearrange("p (c i j) -> p c j i", i=4, j=NJ),
+                rows4.rearrange("p j (c i) -> p c j i", i=4),
+            )
+            return il
+
+        def quant(il, dst):
+            nc.vector.quantize_mx(out=dst[0][:].bitcast(FP8X4), scales=dst[1][:], in_=il[:])
+
+        ilt = {}
+        ilt["x00"] = inter_x("V", 0, 0)
+        ilt["x01"] = inter_x("S", 0, 1)
+        quant(ilt["x00"], xq[(0, 0)])
+        ilt["r0"] = inter("V", a_raw[(0, 0)][:, 0])
+        ilt["r1"] = inter("S", a_raw[(0, 0)][:, 1])
+        quant(ilt["x01"], xq[(0, 1)])
+        quant(ilt["r0"], aq[(0, 0, 0)])
+        ilt["i0"] = inter("V", a_raw[(1, 0)][:, 0])
+        quant(ilt["r1"], aq[(0, 0, 1)])
+        ilt["i1"] = inter("S", a_raw[(1, 0)][:, 1])
+        quant(ilt["i0"], aq[(1, 0, 0)])
+        quant(ilt["i1"], aq[(1, 0, 1)])
+
+        for part in range(2):
+            a_raw[(part, 1)] = raw_tile("a1")
+            load_half(a_raw[(part, 1)], av[part], 1)
+        nc.sync.dma_start(out=wscale[:], in_=scv)
+        load_c(0, 1)
+        w_raw = {}
+        for q in range(2):
+            wt = ring.tile([P, NJ, D], BF16, tag="raw", name="wi", align_bytes=64)
+            nc.sync.dma_start(out=wt[:], in_=wiv[:, q])
+            w_raw[(1, q)] = wt
+        for q in range(2):
+            nc.sync.dma_start(out=wbytes[:, q], in_=wbv[:, q])
+        for r, vec in enumerate((bias, gain, shift)):
+            nc.sync.dma_start(out=rows[0:1, r, :], in_=vec.rearrange("(o e) -> o e", o=1))
+        for h in range(2):
+            nc.sync.dma_start(out=res[:, 4 * h : 4 * h + 4], in_=rv[:, 4 * h : 4 * h + 4])
+        nc.sync.dma_start(out=gain_b[:], in_=gain.partition_broadcast(P))
+        nc.sync.dma_start(out=shift_b[:], in_=shift.partition_broadcast(P))
+
+        def widen(q):
+            wt = ring.tile([P, NJ, D], BF16, tag="raw", name="wr", align_bytes=64)
+            for j in range(NJ):
+                nc.scalar.activation(
+                    out=wt[:, j], in_=wbytes[:, q, j].bitcast(FP8), func=ACT.Copy, scale=wscale[:, q, j : j + 1]
+                )
+            w_raw[(0, q)] = wt
+
+        def chunk_x1(g):
+            return inter_x("S", 1, g), xq[(1, g)]
+
+        def chunk_a1(part, g):
+            return inter("S", a_raw[(part, 1)][:, g]), aq[(part, 1, g)]
+
+        def chunk_w(part, q, e):
+            if part == 0 and e == 0:
+                widen(q)
+            return inter("S", w_raw[(part, q)][:, :, e * HALF : (e + 1) * HALF]), wq[(part, q, e)]
+
+        plan = {
+            0: [(chunk_x1, (0,)), (chunk_x1, (1,))],
+            1: [(chunk_a1, (0, 0))],
+            2: [(chunk_a1, (0, 1)), (chunk_a1, (1, 0)), (chunk_a1, (1, 1))],
+            3: [(chunk_w, (1, 0, 0))],
+            4: [(chunk_w, (1, 0, 1)), (chunk_w, (1, 1, 0))],
+            5: [(chunk_w, (1, 1, 1)), (chunk_w, (0, 0, 0))],
+            6: [(chunk_w, (0, 0, 1))],
+            7: [(chunk_w, (0, 1, 0)), (chunk_w, (0, 1, 1))],
+        }
+
+        groups = [(0, 0), (1, 0), (0, 1), (1, 1), (2, 0), (3, 0), (2, 1), (3, 1)]
+        g_il = {}
+
+        def stage1_unit(k, t):
+            fq, q = groups[k]
+            h, f0 = fq // 2, (fq % 2) * QUART
+            bank = hps.tile([P, 2, QUART], F32, tag="h", name="h")
+            for part in range(2):
+                for g in range(2):
+                    nc.tensor.matmul_mx(
+                        out=bank[:, part],
+                        lhsT=xq[(q, g)][0][:, t * P : (t + 1) * P].bitcast(FP8X4),
+                        lhsT_scale=xq[(q, g)][1][:, t * P : (t + 1) * P],
+                        rhs=aq[(part, h, g)][0][:, f0 : f0 + QUART].bitcast(FP8X4),
+                        rhs_scale=aq[(part, h, g)][1][:, f0 : f0 + QUART],
+                        start=(g == 0),
+                        stop=(g == 1),
+                    )
+            return bank
+
+        def product(k, t, part, bank, dst):
+            fq, q = groups[k]
+            h, f0 = fq // 2, (fq % 2) * QUART
+            nc.vector.tensor_tensor(
+                out=dst[:, t],
+                in0=bank[:, part].unsqueeze(1).broadcast_to([P, 2, QUART]),
+                in1=c_tiles[(q, h)][:, :, t, f0 : f0 + QUART],
+                op=ALU.mult,
+            )
+
+        def filter_sums(k, pa, pb):
+            gr = gpool.tile([P, QUART, NJ], BF16, tag="gr", name="gr", align_bytes=64)
+            gi = gpool.tile([P, QUART, NJ], BF16, tag="gi", name="gi", align_bytes=64)
+            for f in range(0, QUART, P):
+                fs = slice(f, f + P)
+                nc.gpsimd.tensor_tensor(
+                    out=gr[:, fs],
+                    in0=pb[:, :, 1, fs].rearrange("p t f -> p f t"),
+                    in1=pa[:, :, 0, fs].rearrange("p t f -> p f t"),
+                    op=ALU.subtract,
+                )
+            for f in range(0, QUART, P):
+                fs = slice(f, f + P)
+                nc.gpsimd.tensor_tensor(
+                    out=gi[:, fs],
+                    in0=pa[:, :, 1, fs].rearrange("p t f -> p f t"),
+                    in1=pb[:, :, 0, fs].rearrange("p t f -> p f t"),
+                    op=ALU.add,
+                )
+            g_il[k] = (gr, gi)
+
+        def quant_g(k):
+            fq, q = groups[k]
+            for part in range(2):
+                dst = gq[(part, fq, q)]
+                nc.vector.quantize_mx(
+                    out=dst[0][:].bitcast(FP8X4),
+                    scales=dst[1][:],
+                    in_=g_il[k][part][:].rearrange("p f t -> p (f t)"),
+                )
+
+        zu = {}
+
+        def rb_mm(i):
+            banks = []
+            for e in range(2):
+                es = slice(e * HALF, (e + 1) * HALF)
+                bank = yps.tile([P, HALF], F32, tag="y", name="rb")
+                nc.tensor.matmul(out=bank[:], lhsT=ident[:], rhs=res[:, i, es], start=True, stop=False)
+                nc.tensor.matmul(out=bank[:], lhsT=ones[:], rhs=rows[:, 0, es], start=False, stop=True)
+                banks.append(bank)
+            return banks
+
+        def rb_out(i, banks):
+            zt = ring.tile([P, 2, D], F32, tag="raw", name="zu", align_bytes=64)
+            for e in range(2):
+                nc.scalar.copy(out=zt[:, 0, e * HALF : (e + 1) * HALF], in_=banks[e][:])
+            zu[i] = zt
+
+        for k in range(N_GROUPS):
+            if k == 3:
+                load_c(1, 1)
+            pending = [fn(*args) for fn, args in plan[k]]
+            pa = prod.tile([P, NJ, 2, QUART], F32, tag="pa", name="pa")
+            pb = prod.tile([P, NJ, 2, QUART], F32, tag="pb", name="pb")
+            for t in range(NJ):
+                bank = stage1_unit(k, t)
+                product(k, t, 0, bank, pa)
+                if t == NJ - 1:
+                    if k > 0:
+                        quant_g(k - 1)
+                    for il, dst in pending:
+                        quant(il, dst)
+                product(k, t, 1, bank, pb)
+            filter_sums(k, pa, pb)
+
+        for i in range(2):
+            rb_out(i, rb_mm(i))
+
+        spread = []
+        for r in (1, 2):
+            for e in range(2):
+                bank = hps.tile([P, HALF], F32, tag="h", name="spread")
+                nc.tensor.matmul(
+                    out=bank[:], lhsT=ones[:], rhs=rows[:, r, e * HALF : (e + 1) * HALF], start=True, stop=True
+                )
+                spread.append(bank)
+
+        st = keep.tile([P, N_FT, 8], F32, name="st")
+
+        def stat(i, j):
+            return st[:, i, j : j + 1]
+
+        def stage2(i):
+            fq, f0 = i // 2, (i % 2) * P
+            banks = []
+            for e in range(2):
+                bank = yps.tile([P, HALF], F32, tag="y", name="y")
+                n = 0
+                for q in range(2):
+                    for part in (1, 0):
+                        nc.tensor.matmul_mx(
+                            out=bank[:],
+                            lhsT=gq[(part, fq, q)][0][:, f0 : f0 + P].bitcast(FP8X4),
+                            lhsT_scale=gq[(part, fq, q)][1][:, f0 : f0 + P],
+                            rhs=wq[(part, q, e)][0][:].bitcast(FP8X4),
+                            rhs_scale=wq[(part, q, e)][1][:],
+                            start=(n == 0),
+                            stop=(n == 3),
+                        )
+                        n += 1
+                banks.append(bank)
+            return banks
+
+        def finish_z(i, banks):
+            for e in range(2):
+                zs = zu[i][:, 0, e * HALF : (e + 1) * HALF]
+                nc.vector.scalar_tensor_tensor(
+                    out=zs, in0=banks[e][:], scalar=-1.0, in1=zs, op0=ALU.mult, op1=ALU.add, accum_out=stat(i, e)
+                )
+            nc.vector.tensor_scalar(
+                out=stat(i, 2), in0=stat(i, 0), scalar1=stat(i, 1), scalar2=-1.0 / D, op0=ALU.add, op1=ALU.mult
+            )
+
+        def spread_of_z(i):
+            nc.scalar.activation(
+                out=zu[i][:, 1, :], in_=zu[i][:, 0, :], func=ACT.Square, bias=stat(i, 2), accum_out=stat(i, 3)
+            )
+            nc.scalar.activation(out=stat(i, 4), in_=stat(i, 3), func=ACT.Sqrt, scale=1.0 / D)
+
+        def norm_v(i):
+            for e in range(2):
+                es = slice(e * HALF, (e + 1) * HALF)
+                nc.vector.scalar_tensor_tensor(
+                    out=zu[i][:, 1, es],
+                    in0=zu[i][:, 0, es],
+                    scalar=stat(i, 2),
+                    in1=spread[e][:],
+                    op0=ALU.add,
+                    op1=ALU.mult,
+                )
+            nc.vector.reciprocal(out=stat(i, 5), in_=stat(i, 4))
+            for e in range(2):
+                es = slice(e * HALF, (e + 1) * HALF)
+                nc.vector.scalar_tensor_tensor(
+                    out=zu[i][:, 0, es],
+                    in0=zu[i][:, 1, es],
+                    scalar=stat(i, 5),
+                    in1=spread[2 + e][:],
+                    op0=ALU.mult,
+                    op1=ALU.add,
+                )
+
+        def norm_g(i):
+            nc.vector.reciprocal(out=stat(i, 5), in_=stat(i, 4))
+            nc.scalar.activation(out=stat(i, 6), in_=stat(i, 2), func=ACT.Copy, scale=stat(i, 5))
+            nc.scalar.activation(
+                out=zu[i][:, 1, :], in_=zu[i][:, 0, :], func=ACT.Identity, scale=stat(i, 5), bias=stat(i, 6)
+            )
+            nc.gpsimd.tensor_tensor(out=zu[i][:, 0, :], in0=zu[i][:, 1, :], in1=gain_b[:], op=ALU.mult)
+            nc.gpsimd.tensor_tensor(out=zu[i][:, 0, :], in0=zu[i][:, 0, :], in1=shift_b[:], op=ALU.add)
+
+        ov = out.rearrange("(i p) e -> i p e", p=P)
+
+        def finish(i):
+            if i in GP_TILES:
+                norm_g(i)
+            else:
+                norm_v(i)
+            nc.sync.dma_start(out=ov[i], in_=zu[i][:, 0, :])
+
+        for i in range(N_FT):
+            banks = stage2(i)
+            finish_z(i, banks)
+            if i == 1:
+                quant_g(N_GROUPS - 1)
+            if i + 2 < N_FT:
+                rb_out(i + 2, rb_mm(i + 2))
+            spread_of_z(i)
+            if i >= 1:
+                finish(i - 1)
+        finish(N_FT - 1)

@@ -23,7 +23,15 @@ FP8X4 = mybir.dt.float8_e4m3fn_x4
 ALU = mybir.AluOpType
 ACT = mybir.ActivationFunctionType
 
-GP_TILES = (1, 3, 5)
+Z_SLOT = {0: "r3", 1: "r4", 2: "r2", 3: "r0", 4: "r1"}
+H_BANKS = 6
+V_SUM_AFTER = (0, 2, 4, 6)
+QUANT_G_AT = {3: (0, 1), 5: (2, 3), 7: (4, 5)}
+QUANT_G_STEP = {1: (6,), 2: (7,)}
+RB_MM_AT = {5: (0,), 6: (1,)}
+RB_OUT_AT = {5: (0,), 7: (1,)}
+RB_PRE = (2,)
+RB_STEP = {0: (3,), 1: (4,), 2: (5,), 3: (6,), 4: (7,)}
 
 
 def tile_fourier_token_mixer_f4_kernel(
@@ -32,13 +40,12 @@ def tile_fourier_token_mixer_f4_kernel(
     nc = tc.nc
     with ExitStack() as ctx:
         keep = ctx.enter_context(tc.tile_pool(name="keep", bufs=1))
-        ring = ctx.enter_context(tc.tile_pool(name="ring", bufs=5))
+        ring = ctx.enter_context(tc.tile_pool(name="ring", bufs=1))
         cpool = ctx.enter_context(tc.tile_pool(name="cpool", bufs=3))
-        ilpool = ctx.enter_context(tc.tile_pool(name="ilpool", bufs=4))
-        gpool = ctx.enter_context(tc.tile_pool(name="gpool", bufs=2))
-        prod = ctx.enter_context(tc.tile_pool(name="prod", bufs=2))
-        hps = ctx.enter_context(tc.psum_pool(name="hps", bufs=4))
-        yps = ctx.enter_context(tc.psum_pool(name="yps", bufs=4))
+        ilpool = ctx.enter_context(tc.tile_pool(name="ilpool", bufs=5))
+        gpool = ctx.enter_context(tc.tile_pool(name="gpool", bufs=4))
+        prod = ctx.enter_context(tc.tile_pool(name="prod", bufs=4))
+        psum = ctx.enter_context(tc.psum_pool(name="psum", bufs=1))
         ctx.enter_context(tc.manual_schedule())
 
         ident = keep.tile([P, P], BF16, name="ident")
@@ -59,32 +66,46 @@ def tile_fourier_token_mixer_f4_kernel(
         scv = w_re_scale.rearrange("(q p j) o -> p q (j o)", q=2, j=NJ)
         rv = resid.rearrange("(i p) e -> p i e", p=P)
 
-        def raw_tile(name):
-            return ring.tile([P, 2, NJ, HALF], BF16, tag="raw", name=name, align_bytes=64)
+        def raw_tile(tag):
+            return ring.tile([P, 2, NJ, HALF], BF16, tag=tag, name="raw", align_bytes=64)
 
-        def load_half(raw, view, h):
-            for g in range(2):
-                nc.sync.dma_start(out=raw[:, g], in_=view[:, g, :, h * HALF : (h + 1) * HALF])
+        def load(raw, view, g, src, dst, width):
+            nc.sync.dma_start(out=raw[:, g, :, dst : dst + width], in_=view[:, g, :, src : src + width])
 
         c_tiles = {}
 
-        def load_c(q, h):
-            ct = cpool.tile([P, 2, NJ, HALF], BF16, tag="c", name="c")
+        def load_c(q, h, f, width):
             for part in range(2):
-                nc.sync.dma_start(out=ct[:, part], in_=cv[part][:, q, :, h * HALF : (h + 1) * HALF])
-            c_tiles[(q, h)] = ct
+                nc.sync.dma_start(
+                    out=c_tiles[(q, h)][:, part, :, f : f + width],
+                    in_=cv[part][:, q, :, h * HALF + f : h * HALF + f + width],
+                )
 
-        x_raw = []
-        a_raw = {}
-        x_raw.append(raw_tile("x0"))
-        load_half(x_raw[0], xv, 0)
-        for part in range(2):
-            a_raw[(part, 0)] = raw_tile("a0")
-            load_half(a_raw[(part, 0)], av[part], 0)
-        load_c(0, 0)
-        x_raw.append(raw_tile("x1"))
-        load_half(x_raw[1], xv, 1)
-        load_c(1, 0)
+        def c_tile(q, h):
+            c_tiles[(q, h)] = cpool.tile([P, 2, NJ, HALF], BF16, tag="c", name="c")
+
+        x_raw = [raw_tile("r0")]
+        a_raw = {(0, 0): raw_tile("r1"), (1, 0): raw_tile("r2")}
+        for g in range(2):
+            load(x_raw[0], xv, g, 0, 0, HALF)
+        c_tile(0, 0)
+        for f in (0, QUART):
+            for g in range(2):
+                load(a_raw[(0, 0)], av[0], g, f, f, QUART)
+            if f == 0:
+                load_c(0, 0, f, QUART)
+            for g in range(2):
+                load(a_raw[(1, 0)], av[1], g, f, f, QUART)
+            if f > 0:
+                load_c(0, 0, f, QUART)
+        x_raw.append(raw_tile("r3"))
+        for g in range(2):
+            load(x_raw[1], xv, g, HALF, 0, HALF)
+        c_tile(1, 0)
+        load_c(1, 0, 0, HALF)
+        a_raw[(0, 1)] = raw_tile("r4")
+        for g in range(2):
+            load(a_raw[(0, 1)], av[0], g, HALF, 0, HALF)
 
         wscale = keep.tile([P, 2, NJ], F32, name="wscale")
         wbytes = keep.tile([P, 2, NJ, D], U8, name="wbytes")
@@ -98,24 +119,12 @@ def tile_fourier_token_mixer_f4_kernel(
                 keep.tile([P, width], U8, name=name + "_s", align_bytes=64),
             )
 
-        xq = {(q, g): codes_tile("xq%d%d" % (q, g), HALF) for q in range(2) for g in range(2)}
-        aq = {
-            (part, h, g): codes_tile("aq%d%d%d" % (part, h, g), HALF)
-            for part in range(2)
-            for h in range(2)
-            for g in range(2)
-        }
-        wq = {
-            (part, q, e): codes_tile("wq%d%d%d" % (part, q, e), HALF)
-            for part in range(2)
-            for q in range(2)
-            for e in range(2)
-        }
+        two = range(2)
+        xq = {(q, g): codes_tile("xq%d%d" % (q, g), HALF) for q in two for g in two}
+        aq = {(part, h, g): codes_tile("aq%d%d%d" % (part, h, g), HALF) for part in two for h in two for g in two}
+        wq = {(part, q, e): codes_tile("wq%d%d%d" % (part, q, e), HALF) for part in two for q in two for e in two}
         gq = {
-            (part, fq, q): codes_tile("gq%d%d%d" % (part, fq, q), QUART)
-            for part in range(2)
-            for fq in range(4)
-            for q in range(2)
+            (part, fq, q): codes_tile("gq%d%d%d" % (part, fq, q), QUART) for part in two for fq in range(4) for q in two
         }
 
         def il_tile():
@@ -138,56 +147,32 @@ def tile_fourier_token_mixer_f4_kernel(
 
         def inter(eng, rows4):
             il = il_tile()
+            width = rows4.shape[2]
             copy_on(
                 eng,
-                il[:].rearrange("p (c i j) -> p c j i", i=4, j=NJ),
+                il[:, 0 : NJ * width].rearrange("p (c i j) -> p c j i", i=4, j=NJ),
                 rows4.rearrange("p j (c i) -> p c j i", i=4),
             )
             return il
 
-        def quant(il, dst):
-            nc.vector.quantize_mx(out=dst[0][:].bitcast(FP8X4), scales=dst[1][:], in_=il[:])
+        def quant(il, dst, f=0, width=HALF):
+            nc.vector.quantize_mx(
+                out=dst[0][:, f : f + width].bitcast(FP8X4), scales=dst[1][:, f : f + width], in_=il[:, 0 : NJ * width]
+            )
 
-        ilt = {}
-        ilt["x00"] = inter_x("V", 0, 0)
-        ilt["x01"] = inter_x("S", 0, 1)
-        quant(ilt["x00"], xq[(0, 0)])
-        ilt["r0"] = inter("V", a_raw[(0, 0)][:, 0])
-        ilt["r1"] = inter("S", a_raw[(0, 0)][:, 1])
-        quant(ilt["x01"], xq[(0, 1)])
-        quant(ilt["r0"], aq[(0, 0, 0)])
-        ilt["i0"] = inter("V", a_raw[(1, 0)][:, 0])
-        quant(ilt["r1"], aq[(0, 0, 1)])
-        ilt["i1"] = inter("S", a_raw[(1, 0)][:, 1])
-        quant(ilt["i0"], aq[(1, 0, 0)])
-        quant(ilt["i1"], aq[(1, 0, 1)])
-
-        for part in range(2):
-            a_raw[(part, 1)] = raw_tile("a1")
-            load_half(a_raw[(part, 1)], av[part], 1)
-        nc.sync.dma_start(out=wscale[:], in_=scv)
-        load_c(0, 1)
-        w_raw = {}
-        for q in range(2):
-            wt = ring.tile([P, NJ, D], BF16, tag="raw", name="wi", align_bytes=64)
-            nc.sync.dma_start(out=wt[:], in_=wiv[:, q])
-            w_raw[(1, q)] = wt
-        for q in range(2):
-            nc.sync.dma_start(out=wbytes[:, q], in_=wbv[:, q])
-        for r, vec in enumerate((bias, gain, shift)):
-            nc.sync.dma_start(out=rows[0:1, r, :], in_=vec.rearrange("(o e) -> o e", o=1))
-        for h in range(2):
-            nc.sync.dma_start(out=res[:, 4 * h : 4 * h + 4], in_=rv[:, 4 * h : 4 * h + 4])
-        nc.sync.dma_start(out=gain_b[:], in_=gain.partition_broadcast(P))
-        nc.sync.dma_start(out=shift_b[:], in_=shift.partition_broadcast(P))
+        def inter_a0(eng, part, g, f):
+            return inter(eng, a_raw[(part, 0)][:, g, :, f : f + QUART])
 
         def widen(q):
-            wt = ring.tile([P, NJ, D], BF16, tag="raw", name="wr", align_bytes=64)
+            wt = ring.tile([P, NJ, D], BF16, tag="r%d" % q, name="wr", align_bytes=64)
             for j in range(NJ):
                 nc.scalar.activation(
                     out=wt[:, j], in_=wbytes[:, q, j].bitcast(FP8), func=ACT.Copy, scale=wscale[:, q, j : j + 1]
                 )
             w_raw[(0, q)] = wt
+
+        def chunk_a0(eng, part, g, f):
+            return inter_a0(eng, part, g, f), aq[(part, 0, g)], f, QUART
 
         def chunk_x1(g):
             return inter_x("S", 1, g), xq[(1, g)]
@@ -195,72 +180,85 @@ def tile_fourier_token_mixer_f4_kernel(
         def chunk_a1(part, g):
             return inter("S", a_raw[(part, 1)][:, g]), aq[(part, 1, g)]
 
+        w_raw = {}
+
         def chunk_w(part, q, e):
             if part == 0 and e == 0:
                 widen(q)
             return inter("S", w_raw[(part, q)][:, :, e * HALF : (e + 1) * HALF]), wq[(part, q, e)]
 
-        plan = {
-            0: [(chunk_x1, (0,)), (chunk_x1, (1,))],
-            1: [(chunk_a1, (0, 0))],
-            2: [(chunk_a1, (0, 1)), (chunk_a1, (1, 0)), (chunk_a1, (1, 1))],
-            3: [(chunk_w, (1, 0, 0))],
-            4: [(chunk_w, (1, 0, 1)), (chunk_w, (1, 1, 0))],
-            5: [(chunk_w, (1, 1, 1)), (chunk_w, (0, 0, 0))],
-            6: [(chunk_w, (0, 0, 1))],
-            7: [(chunk_w, (0, 1, 0)), (chunk_w, (0, 1, 1))],
-        }
+        xi0 = inter_x("V", 0, 0)
+        xi1 = inter_x("S", 0, 1)
+        quant(xi0, xq[(0, 0)])
+        re0 = inter_a0("V", 0, 0, 0)
+        re1 = inter_a0("S", 0, 1, 0)
+        quant(xi1, xq[(0, 1)])
+        quant(re0, aq[(0, 0, 0)], 0, QUART)
+        quant(re1, aq[(0, 0, 1)], 0, QUART)
+        a_raw[(1, 1)] = raw_tile("r0")
+        for g in range(2):
+            load(a_raw[(1, 1)], av[1], g, HALF, 0, HALF)
+        nc.sync.dma_start(out=wscale[:], in_=scv)
+        for q in range(2):
+            wt = ring.tile([P, NJ, D], BF16, tag="r%d" % (1 + q), name="wi", align_bytes=64)
+            w_raw[(1, q)] = wt
+        c_tile(0, 1)
+        load_c(0, 1, 0, HALF)
+
+        def late_loads():
+            for q in range(2):
+                nc.sync.dma_start(out=w_raw[(1, q)][:], in_=wiv[:, q])
+            for r, vec in enumerate((bias, gain, shift)):
+                nc.sync.dma_start(out=rows[0:1, r, :], in_=vec.rearrange("(o e) -> o e", o=1))
+            nc.sync.dma_start(out=res[:, 0:4], in_=rv[:, 0:4])
+            for q in range(2):
+                nc.sync.dma_start(out=wbytes[:, q], in_=wbv[:, q])
+            nc.sync.dma_start(out=res[:, 4:8], in_=rv[:, 4:8])
+            nc.sync.dma_start(out=gain_b[:], in_=gain.partition_broadcast(P))
+            nc.sync.dma_start(out=shift_b[:], in_=shift.partition_broadcast(P))
 
         groups = [(0, 0), (1, 0), (0, 1), (1, 1), (2, 0), (3, 0), (2, 1), (3, 1)]
         g_il = {}
 
-        def stage1_unit(k, t):
+        def bank_tile(b, shape, name):
+            return psum.tile(shape, F32, tag="b%d" % b, name=name)
+
+        def stage1(k, part, s):
             fq, q = groups[k]
-            h, f0 = fq // 2, (fq % 2) * QUART
-            bank = hps.tile([P, 2, QUART], F32, tag="h", name="h")
-            for part in range(2):
+            h, f0 = fq // 2, (fq % 2) * QUART + s * P
+            bank = bank_tile((4 * k + 2 * part + s) % H_BANKS, [P, NJ, P], "h")
+            for t in range(NJ):
                 for g in range(2):
                     nc.tensor.matmul_mx(
-                        out=bank[:, part],
+                        out=bank[:, t],
                         lhsT=xq[(q, g)][0][:, t * P : (t + 1) * P].bitcast(FP8X4),
                         lhsT_scale=xq[(q, g)][1][:, t * P : (t + 1) * P],
-                        rhs=aq[(part, h, g)][0][:, f0 : f0 + QUART].bitcast(FP8X4),
-                        rhs_scale=aq[(part, h, g)][1][:, f0 : f0 + QUART],
+                        rhs=aq[(part, h, g)][0][:, f0 : f0 + P].bitcast(FP8X4),
+                        rhs_scale=aq[(part, h, g)][1][:, f0 : f0 + P],
                         start=(g == 0),
                         stop=(g == 1),
                     )
             return bank
 
-        def product(k, t, part, bank, dst):
+        def product(k, part, s, bank):
             fq, q = groups[k]
-            h, f0 = fq // 2, (fq % 2) * QUART
+            h, f0 = fq // 2, (fq % 2) * QUART + s * P
+            dst = prod.tile([P, 2, P, NJ], F32, tag="p%d" % part, name="prod")
             nc.vector.tensor_tensor(
-                out=dst[:, t],
-                in0=bank[:, part].unsqueeze(1).broadcast_to([P, 2, QUART]),
-                in1=c_tiles[(q, h)][:, :, t, f0 : f0 + QUART],
+                out=dst[:],
+                in0=bank[:].rearrange("p t f -> p f t").unsqueeze(1).broadcast_to([P, 2, P, NJ]),
+                in1=c_tiles[(q, h)][:, :, :, f0 - 0 : f0 + P].rearrange("p c t f -> p c f t"),
                 op=ALU.mult,
             )
+            return dst
 
-        def filter_sums(k, pa, pb):
-            gr = gpool.tile([P, QUART, NJ], BF16, tag="gr", name="gr", align_bytes=64)
-            gi = gpool.tile([P, QUART, NJ], BF16, tag="gi", name="gi", align_bytes=64)
-            for f in range(0, QUART, P):
-                fs = slice(f, f + P)
-                nc.gpsimd.tensor_tensor(
-                    out=gr[:, fs],
-                    in0=pb[:, :, 1, fs].rearrange("p t f -> p f t"),
-                    in1=pa[:, :, 0, fs].rearrange("p t f -> p f t"),
-                    op=ALU.subtract,
-                )
-            for f in range(0, QUART, P):
-                fs = slice(f, f + P)
-                nc.gpsimd.tensor_tensor(
-                    out=gi[:, fs],
-                    in0=pa[:, :, 1, fs].rearrange("p t f -> p f t"),
-                    in1=pb[:, :, 0, fs].rearrange("p t f -> p f t"),
-                    op=ALU.add,
-                )
-            g_il[k] = (gr, gi)
+        def g_re_sum(eng, k, s, pa, pb):
+            fs = slice(s * P, (s + 1) * P)
+            eng.tensor_tensor(out=g_il[k][0][:, fs], in0=pb[:, 1], in1=pa[:, 0], op=ALU.subtract)
+
+        def g_im_sum(eng, k, s, pa, pb):
+            fs = slice(s * P, (s + 1) * P)
+            eng.tensor_tensor(out=g_il[k][1][:, fs], in0=pa[:, 1], in1=pb[:, 0], op=ALU.add)
 
         def quant_g(k):
             fq, q = groups[k]
@@ -274,50 +272,72 @@ def tile_fourier_token_mixer_f4_kernel(
 
         zu = {}
 
+        rb_banks = {}
+
         def rb_mm(i):
-            banks = []
+            rb_banks[i] = []
             for e in range(2):
                 es = slice(e * HALF, (e + 1) * HALF)
-                bank = yps.tile([P, HALF], F32, tag="y", name="rb")
+                bank = bank_tile(6 + e, [P, HALF], "rb")
                 nc.tensor.matmul(out=bank[:], lhsT=ident[:], rhs=res[:, i, es], start=True, stop=False)
                 nc.tensor.matmul(out=bank[:], lhsT=ones[:], rhs=rows[:, 0, es], start=False, stop=True)
-                banks.append(bank)
-            return banks
+                rb_banks[i].append(bank)
 
-        def rb_out(i, banks):
-            zt = ring.tile([P, 2, D], F32, tag="raw", name="zu", align_bytes=64)
+        def rb_out(i):
+            if i in Z_SLOT:
+                zt = ring.tile([P, 2, D], F32, tag=Z_SLOT[i], name="zu", align_bytes=64)
+                zu[i] = (zt[:, 0], zt[:, 1])
+            else:
+                za = prod.tile([P, D], F32, tag="p0", name="za")
+                ua = prod.tile([P, D], F32, tag="p1", name="ua")
+                zu[i] = (za[:], ua[:])
             for e in range(2):
-                nc.scalar.copy(out=zt[:, 0, e * HALF : (e + 1) * HALF], in_=banks[e][:])
-            zu[i] = zt
+                nc.scalar.copy(out=zu[i][0][:, e * HALF : (e + 1) * HALF], in_=rb_banks[i][e][:])
 
+        plan = {
+            0: [(chunk_a0, ("S", 1, 1, 0)), (chunk_a0, ("S", 0, 1, QUART)), (chunk_a0, ("S", 1, 1, QUART))],
+            1: [(chunk_x1, (0,)), (chunk_x1, (1,))],
+            3: [(chunk_a1, (0, 0)), (chunk_a1, (0, 1)), (chunk_a1, (1, 0)), (chunk_a1, (1, 1))],
+            5: [(chunk_w, (1, 0, 0)), (chunk_w, (1, 0, 1)), (chunk_w, (1, 1, 0)), (chunk_w, (1, 1, 1))],
+            7: [(chunk_w, (0, 0, 0)), (chunk_w, (0, 0, 1)), (chunk_w, (0, 1, 0)), (chunk_w, (0, 1, 1))],
+        }
+        v_plan = {0: [(chunk_a0, ("V", 1, 0, 0)), (chunk_a0, ("V", 0, 0, QUART)), (chunk_a0, ("V", 1, 0, QUART))]}
+
+        deferred = []
         for k in range(N_GROUPS):
+            if k == 2:
+                late_loads()
             if k == 3:
-                load_c(1, 1)
-            pending = [fn(*args) for fn, args in plan[k]]
-            pa = prod.tile([P, NJ, 2, QUART], F32, tag="pa", name="pa")
-            pb = prod.tile([P, NJ, 2, QUART], F32, tag="pb", name="pb")
-            for t in range(NJ):
-                bank = stage1_unit(k, t)
-                product(k, t, 0, bank, pa)
-                if t == NJ - 1:
-                    if k > 0:
-                        quant_g(k - 1)
-                    for il, dst in pending:
-                        quant(il, dst)
-                product(k, t, 1, bank, pb)
-            filter_sums(k, pa, pb)
-
-        for i in range(2):
-            rb_out(i, rb_mm(i))
-
-        spread = []
-        for r in (1, 2):
-            for e in range(2):
-                bank = hps.tile([P, HALF], F32, tag="h", name="spread")
-                nc.tensor.matmul(
-                    out=bank[:], lhsT=ones[:], rhs=rows[:, r, e * HALF : (e + 1) * HALF], start=True, stop=True
-                )
-                spread.append(bank)
+                c_tile(1, 1)
+                load_c(1, 1, 0, HALF)
+            gr = gpool.tile([P, QUART, NJ], BF16, tag="gr", name="gr", align_bytes=64)
+            gi = gpool.tile([P, QUART, NJ], BF16, tag="gi", name="gi", align_bytes=64)
+            g_il[k] = (gr, gi)
+            for i in RB_MM_AT.get(k, ()):
+                rb_mm(i)
+            pending = [fn(*args) for fn, args in plan.get(k, ())]
+            for i in RB_OUT_AT.get(k, ()):
+                rb_out(i)
+            banks = [stage1(k, 0, s) for s in two]
+            pa = [product(k, 0, s, banks[s]) for s in two]
+            while deferred:
+                g_im_sum(nc.vector, *deferred.pop())
+            for g_done in QUANT_G_AT.get(k, ()):
+                quant_g(g_done)
+            for n, (fn, args) in enumerate(v_plan.get(k, ())):
+                if n == 2:
+                    quant(*pending.pop(0))
+                pending.append(fn(*args))
+            for item in pending:
+                quant(*item)
+            banks = [stage1(k, 1, s) for s in two]
+            for s in two:
+                pb = product(k, 1, s, banks[s])
+                g_re_sum(nc.gpsimd, k, s, pa[s], pb)
+                if s == 1 and k in V_SUM_AFTER:
+                    deferred.append((k, s, pa[s], pb))
+                else:
+                    g_im_sum(nc.gpsimd, k, s, pa[s], pb)
 
         st = keep.tile([P, N_FT, 8], F32, name="st")
 
@@ -328,7 +348,7 @@ def tile_fourier_token_mixer_f4_kernel(
             fq, f0 = i // 2, (i % 2) * P
             banks = []
             for e in range(2):
-                bank = yps.tile([P, HALF], F32, tag="y", name="y")
+                bank = bank_tile(2 + 2 * (i % 2) + e, [P, HALF], "y")
                 n = 0
                 for q in range(2):
                     for part in (1, 0):
@@ -345,71 +365,98 @@ def tile_fourier_token_mixer_f4_kernel(
                 banks.append(bank)
             return banks
 
-        def finish_z(i, banks):
-            for e in range(2):
-                zs = zu[i][:, 0, e * HALF : (e + 1) * HALF]
-                nc.vector.scalar_tensor_tensor(
-                    out=zs, in0=banks[e][:], scalar=-1.0, in1=zs, op0=ALU.mult, op1=ALU.add, accum_out=stat(i, e)
-                )
+        def finish_z(i, e, banks):
+            zs = zu[i][0][:, e * HALF : (e + 1) * HALF]
+            nc.vector.scalar_tensor_tensor(
+                out=zs, in0=banks[e][:], scalar=-1.0, in1=zs, op0=ALU.mult, op1=ALU.add, accum_out=stat(i, e)
+            )
+
+        def neg_mean(i):
             nc.vector.tensor_scalar(
                 out=stat(i, 2), in0=stat(i, 0), scalar1=stat(i, 1), scalar2=-1.0 / D, op0=ALU.add, op1=ALU.mult
             )
 
         def spread_of_z(i):
-            nc.scalar.activation(
-                out=zu[i][:, 1, :], in_=zu[i][:, 0, :], func=ACT.Square, bias=stat(i, 2), accum_out=stat(i, 3)
-            )
+            z, u = zu[i]
+            nc.scalar.activation(out=u, in_=z, func=ACT.Square, bias=stat(i, 2), accum_out=stat(i, 3))
             nc.scalar.activation(out=stat(i, 4), in_=stat(i, 3), func=ACT.Sqrt, scale=1.0 / D)
 
-        def norm_v(i):
-            for e in range(2):
-                es = slice(e * HALF, (e + 1) * HALF)
-                nc.vector.scalar_tensor_tensor(
-                    out=zu[i][:, 1, es],
-                    in0=zu[i][:, 0, es],
-                    scalar=stat(i, 2),
-                    in1=spread[e][:],
-                    op0=ALU.add,
-                    op1=ALU.mult,
-                )
+        def rstd(i):
             nc.vector.reciprocal(out=stat(i, 5), in_=stat(i, 4))
-            for e in range(2):
-                es = slice(e * HALF, (e + 1) * HALF)
-                nc.vector.scalar_tensor_tensor(
-                    out=zu[i][:, 0, es],
-                    in0=zu[i][:, 1, es],
-                    scalar=stat(i, 5),
-                    in1=spread[2 + e][:],
-                    op0=ALU.mult,
-                    op1=ALU.add,
-                )
-
-        def norm_g(i):
-            nc.vector.reciprocal(out=stat(i, 5), in_=stat(i, 4))
-            nc.scalar.activation(out=stat(i, 6), in_=stat(i, 2), func=ACT.Copy, scale=stat(i, 5))
-            nc.scalar.activation(
-                out=zu[i][:, 1, :], in_=zu[i][:, 0, :], func=ACT.Identity, scale=stat(i, 5), bias=stat(i, 6)
-            )
-            nc.gpsimd.tensor_tensor(out=zu[i][:, 0, :], in0=zu[i][:, 1, :], in1=gain_b[:], op=ALU.mult)
-            nc.gpsimd.tensor_tensor(out=zu[i][:, 0, :], in0=zu[i][:, 0, :], in1=shift_b[:], op=ALU.add)
 
         ov = out.rearrange("(i p) e -> i p e", p=P)
 
-        def finish(i):
-            if i in GP_TILES:
-                norm_g(i)
-            else:
-                norm_v(i)
-            nc.sync.dma_start(out=ov[i], in_=zu[i][:, 0, :])
+        def store(i, e):
+            es = slice(e * HALF, (e + 1) * HALF)
+            nc.sync.dma_start(out=ov[i][:, es], in_=zu[i][0][:, es])
 
+        def scale_v(i, e):
+            z, u = zu[i]
+            es = slice(e * HALF, (e + 1) * HALF)
+            nc.vector.scalar_tensor_tensor(
+                out=u[:, es],
+                in0=z[:, es],
+                scalar=stat(i, 2),
+                in1=spread[0][:] if e == 1 else gain_b[:, es],
+                op0=ALU.add,
+                op1=ALU.mult,
+            )
+
+        def shift_v(i, e):
+            z, u = zu[i]
+            es = slice(e * HALF, (e + 1) * HALF)
+            nc.vector.scalar_tensor_tensor(
+                out=z[:, es],
+                in0=u[:, es],
+                scalar=stat(i, 5),
+                in1=spread[1][:] if e == 1 else shift_b[:, es],
+                op0=ALU.mult,
+                op1=ALU.add,
+            )
+            store(i, e)
+
+        def normalize_g(i):
+            z, u = zu[i]
+            es = slice(0, HALF)
+            nc.scalar.activation(out=stat(i, 6), in_=stat(i, 2), func=ACT.Copy, scale=stat(i, 5))
+            nc.scalar.activation(out=u[:, es], in_=z[:, es], func=ACT.Identity, scale=stat(i, 5), bias=stat(i, 6))
+            nc.gpsimd.tensor_tensor(out=z[:, es], in0=u[:, es], in1=gain_b[:, es], op=ALU.mult)
+            nc.gpsimd.tensor_tensor(out=z[:, es], in0=z[:, es], in1=shift_b[:, es], op=ALU.add)
+            store(i, 0)
+
+        y_banks = {}
+        for i in RB_PRE:
+            rb_mm(i)
+            rb_out(i)
+        for i in range(2):
+            y_banks[i] = stage2(i)
+        spread = []
+        for r in (1, 2):
+            bank = bank_tile(r - 1, [P, HALF], "spread")
+            nc.tensor.matmul(out=bank[:], lhsT=ones[:], rhs=rows[:, r, HALF:D], start=True, stop=True)
+            spread.append(bank)
         for i in range(N_FT):
-            banks = stage2(i)
-            finish_z(i, banks)
-            if i == 1:
-                quant_g(N_GROUPS - 1)
+            finish_z(i, 0, y_banks[i])
+            finish_z(i, 1, y_banks[i])
+            for j in RB_STEP.get(i, ()):
+                rb_mm(j)
             if i + 2 < N_FT:
-                rb_out(i + 2, rb_mm(i + 2))
-            spread_of_z(i)
+                y_banks[i + 2] = stage2(i + 2)
             if i >= 1:
-                finish(i - 1)
-        finish(N_FT - 1)
+                scale_v(i - 1, 1)
+                rstd(i - 1)
+            neg_mean(i)
+            spread_of_z(i)
+            for j in RB_STEP.get(i, ()):
+                rb_out(j)
+            if i >= 1:
+                shift_v(i - 1, 1)
+                normalize_g(i - 1)
+            for g_done in QUANT_G_STEP.get(i, ()):
+                quant_g(g_done)
+        i = N_FT - 1
+        scale_v(i, 1)
+        scale_v(i, 0)
+        rstd(i)
+        shift_v(i, 1)
+        shift_v(i, 0)

@@ -30,8 +30,10 @@ QUANT_G_AT = {3: (0, 1), 5: (2, 3), 7: (4, 5)}
 QUANT_G_STEP = {1: (6,), 2: (7,)}
 RB_MM_AT = {5: (0,), 6: (1,)}
 RB_OUT_AT = {5: (0,), 7: (1,)}
-RB_PRE = (2,)
-RB_STEP = {0: (3,), 1: (4,), 2: (5,), 3: (6,), 4: (7,)}
+RB_PRE = ((2, 4), (3, 6), (4, 2))
+G_TILES = (0, 1, 2, 3, 4, 5)
+SPREAD_STEP = 4
+RB_STEP = {1: (5,), 2: (6,), 3: (7,)}
 
 
 def tile_fourier_token_mixer_f4_kernel(
@@ -53,7 +55,7 @@ def tile_fourier_token_mixer_f4_kernel(
         rows = keep.tile([P, 3, D], BF16, name="rows")
         tiny = keep.tile([P, 1], F32, name="tiny")
         nc.gpsimd.memset(tiny[:], 1.0)
-        nc.scalar.activation(out=tiny[:], in_=tiny[:], func=ACT.Sqrt)
+        nc.scalar.activation(out=tiny[:], in_=tiny[:], func=ACT.Abs_reciprocal_sqrt)
         make_identity(nc, ident[:])
         nc.gpsimd.memset(ones[:], 1.0)
         nc.gpsimd.memset(rows[:], 0.0)
@@ -188,10 +190,10 @@ def tile_fourier_token_mixer_f4_kernel(
             return inter("S", w_raw[(part, q)][:, :, e * HALF : (e + 1) * HALF]), wq[(part, q, e)]
 
         xi0 = inter_x("V", 0, 0)
-        xi1 = inter_x("S", 0, 1)
-        quant(xi0, xq[(0, 0)])
-        re0 = inter_a0("V", 0, 0, 0)
+        xi1 = inter_x("V", 0, 1)
+        re0 = inter_a0("S", 0, 0, 0)
         re1 = inter_a0("S", 0, 1, 0)
+        quant(xi0, xq[(0, 0)])
         quant(xi1, xq[(0, 1)])
         quant(re0, aq[(0, 0, 0)], 0, QUART)
         quant(re1, aq[(0, 0, 1)], 0, QUART)
@@ -274,11 +276,11 @@ def tile_fourier_token_mixer_f4_kernel(
 
         rb_banks = {}
 
-        def rb_mm(i):
+        def rb_mm(i, b=6):
             rb_banks[i] = []
             for e in range(2):
                 es = slice(e * HALF, (e + 1) * HALF)
-                bank = bank_tile(6 + e, [P, HALF], "rb")
+                bank = bank_tile(b + e, [P, HALF], "rb")
                 nc.tensor.matmul(out=bank[:], lhsT=ident[:], rhs=res[:, i, es], start=True, stop=False)
                 nc.tensor.matmul(out=bank[:], lhsT=ones[:], rhs=rows[:, 0, es], start=False, stop=True)
                 rb_banks[i].append(bank)
@@ -299,8 +301,9 @@ def tile_fourier_token_mixer_f4_kernel(
             1: [(chunk_x1, (0,)), (chunk_x1, (1,))],
             3: [(chunk_a1, (0, 0)), (chunk_a1, (0, 1)), (chunk_a1, (1, 0)), (chunk_a1, (1, 1))],
             5: [(chunk_w, (1, 0, 0)), (chunk_w, (1, 0, 1)), (chunk_w, (1, 1, 0)), (chunk_w, (1, 1, 1))],
-            7: [(chunk_w, (0, 0, 0)), (chunk_w, (0, 0, 1)), (chunk_w, (0, 1, 0)), (chunk_w, (0, 1, 1))],
+            7: [(chunk_w, (0, 0, 0)), (chunk_w, (0, 0, 1)), (chunk_w, (0, 1, 0))],
         }
+        plan2 = {7: [(chunk_w, (0, 1, 1))]}
         v_plan = {0: [(chunk_a0, ("V", 1, 0, 0)), (chunk_a0, ("V", 0, 0, QUART)), (chunk_a0, ("V", 1, 0, QUART))]}
 
         deferred = []
@@ -318,6 +321,7 @@ def tile_fourier_token_mixer_f4_kernel(
             pending = [fn(*args) for fn, args in plan.get(k, ())]
             for i in RB_OUT_AT.get(k, ()):
                 rb_out(i)
+            pending += [fn(*args) for fn, args in plan2.get(k, ())]
             banks = [stage1(k, 0, s) for s in two]
             pa = [product(k, 0, s, banks[s]) for s in two]
             while deferred:
@@ -348,7 +352,7 @@ def tile_fourier_token_mixer_f4_kernel(
             fq, f0 = i // 2, (i % 2) * P
             banks = []
             for e in range(2):
-                bank = bank_tile(2 + 2 * (i % 2) + e, [P, HALF], "y")
+                bank = bank_tile(4 + 2 * (i % 2) + e, [P, HALF], "y")
                 n = 0
                 for q in range(2):
                     for part in (1, 0):
@@ -379,10 +383,7 @@ def tile_fourier_token_mixer_f4_kernel(
         def spread_of_z(i):
             z, u = zu[i]
             nc.scalar.activation(out=u, in_=z, func=ACT.Square, bias=stat(i, 2), accum_out=stat(i, 3))
-            nc.scalar.activation(out=stat(i, 4), in_=stat(i, 3), func=ACT.Sqrt, scale=1.0 / D)
-
-        def rstd(i):
-            nc.vector.reciprocal(out=stat(i, 5), in_=stat(i, 4))
+            nc.scalar.activation(out=stat(i, 5), in_=stat(i, 3), func=ACT.Abs_reciprocal_sqrt, scale=1.0 / D)
 
         ov = out.rearrange("(i p) e -> i p e", p=P)
 
@@ -397,7 +398,7 @@ def tile_fourier_token_mixer_f4_kernel(
                 out=u[:, es],
                 in0=z[:, es],
                 scalar=stat(i, 2),
-                in1=spread[0][:] if e == 1 else gain_b[:, es],
+                in1=spread[(1, e)][:],
                 op0=ALU.add,
                 op1=ALU.mult,
             )
@@ -409,7 +410,7 @@ def tile_fourier_token_mixer_f4_kernel(
                 out=z[:, es],
                 in0=u[:, es],
                 scalar=stat(i, 5),
-                in1=spread[1][:] if e == 1 else shift_b[:, es],
+                in1=spread[(2, e)][:],
                 op0=ALU.mult,
                 op1=ALU.add,
             )
@@ -424,39 +425,52 @@ def tile_fourier_token_mixer_f4_kernel(
             nc.gpsimd.tensor_tensor(out=z[:, es], in0=z[:, es], in1=shift_b[:, es], op=ALU.add)
             store(i, 0)
 
+        def v_halves(i):
+            return (1,) if i in G_TILES else (1, 0)
+
         y_banks = {}
-        for i in RB_PRE:
-            rb_mm(i)
+        for i, b in RB_PRE:
+            rb_mm(i, b)
             rb_out(i)
         for i in range(2):
             y_banks[i] = stage2(i)
-        spread = []
+        spread = {}
+
+        def spread_mm(r, e, b):
+            bank = bank_tile(b, [P, HALF], "spread")
+            nc.tensor.matmul(
+                out=bank[:], lhsT=ones[:], rhs=rows[:, r, e * HALF : (e + 1) * HALF], start=True, stop=True
+            )
+            spread[(r, e)] = bank
+
         for r in (1, 2):
-            bank = bank_tile(r - 1, [P, HALF], "spread")
-            nc.tensor.matmul(out=bank[:], lhsT=ones[:], rhs=rows[:, r, HALF:D], start=True, stop=True)
-            spread.append(bank)
+            spread_mm(r, 1, r - 1)
         for i in range(N_FT):
             finish_z(i, 0, y_banks[i])
             finish_z(i, 1, y_banks[i])
             for j in RB_STEP.get(i, ()):
-                rb_mm(j)
+                rb_mm(j, 2)
             if i + 2 < N_FT:
                 y_banks[i + 2] = stage2(i + 2)
             if i >= 1:
-                scale_v(i - 1, 1)
-                rstd(i - 1)
+                for e in v_halves(i - 1):
+                    scale_v(i - 1, e)
             neg_mean(i)
             spread_of_z(i)
             for j in RB_STEP.get(i, ()):
                 rb_out(j)
+            if i == SPREAD_STEP:
+                for r in (1, 2):
+                    spread_mm(r, 0, r + 1)
             if i >= 1:
-                shift_v(i - 1, 1)
-                normalize_g(i - 1)
+                for e in v_halves(i - 1):
+                    shift_v(i - 1, e)
+                if i - 1 in G_TILES:
+                    normalize_g(i - 1)
             for g_done in QUANT_G_STEP.get(i, ()):
                 quant_g(g_done)
         i = N_FT - 1
         scale_v(i, 1)
         scale_v(i, 0)
-        rstd(i)
         shift_v(i, 1)
         shift_v(i, 0)

@@ -25,13 +25,13 @@ ACT = mybir.ActivationFunctionType
 
 Z_SLOT = {0: "r3", 1: "r4", 2: "r2", 3: "r0", 4: "r1"}
 H_BANKS = 6
-V_SUM_AFTER = (0, 2, 4, 6)
-QUANT_G_AT = {3: (0, 1), 5: (2, 3), 7: (4, 5)}
-QUANT_G_STEP = {1: (6,), 2: (7,)}
+V_SUMS = ((3,),) * 8
+QUANT_G_STEP = {1: (7,)}
 RB_MM_AT = {5: (0,), 6: (1,)}
 RB_OUT_AT = {5: (0,), 7: (1,)}
 RB_PRE = ((2, 4), (3, 6), (4, 2))
-G_TILES = (0, 1, 2, 3, 4, 5)
+G_TILES = (0, 1, 2, 3, 4)
+G_LAG = 3
 SPREAD_STEP = 4
 RB_STEP = {1: (5,), 2: (6,), 3: (7,)}
 
@@ -44,8 +44,8 @@ def tile_fourier_token_mixer_f4_kernel(
         keep = ctx.enter_context(tc.tile_pool(name="keep", bufs=1))
         ring = ctx.enter_context(tc.tile_pool(name="ring", bufs=1))
         cpool = ctx.enter_context(tc.tile_pool(name="cpool", bufs=3))
-        ilpool = ctx.enter_context(tc.tile_pool(name="ilpool", bufs=5))
-        gpool = ctx.enter_context(tc.tile_pool(name="gpool", bufs=4))
+        ilpool = ctx.enter_context(tc.tile_pool(name="ilpool", bufs=7))
+        gpool = ctx.enter_context(tc.tile_pool(name="gpool", bufs=1))
         prod = ctx.enter_context(tc.tile_pool(name="prod", bufs=4))
         psum = ctx.enter_context(tc.psum_pool(name="psum", bufs=1))
         ctx.enter_context(tc.manual_schedule())
@@ -299,23 +299,22 @@ def tile_fourier_token_mixer_f4_kernel(
         plan = {
             0: [(chunk_a0, ("S", 1, 1, 0)), (chunk_a0, ("S", 0, 1, QUART)), (chunk_a0, ("S", 1, 1, QUART))],
             1: [(chunk_x1, (0,)), (chunk_x1, (1,))],
-            3: [(chunk_a1, (0, 0)), (chunk_a1, (0, 1)), (chunk_a1, (1, 0)), (chunk_a1, (1, 1))],
-            5: [(chunk_w, (1, 0, 0)), (chunk_w, (1, 0, 1)), (chunk_w, (1, 1, 0)), (chunk_w, (1, 1, 1))],
-            7: [(chunk_w, (0, 0, 0)), (chunk_w, (0, 0, 1)), (chunk_w, (0, 1, 0))],
+            2: [(chunk_a1, (0, 0))],
+            3: [(chunk_a1, (0, 1)), (chunk_a1, (1, 0)), (chunk_a1, (1, 1))],
+            4: [(chunk_w, (1, 0, 0))],
+            5: [(chunk_w, (1, 0, 1)), (chunk_w, (1, 1, 0)), (chunk_w, (1, 1, 1))],
+            6: [(chunk_w, (0, 0, 0)), (chunk_w, (0, 0, 1))],
+            7: [(chunk_w, (0, 1, 0))],
         }
         plan2 = {7: [(chunk_w, (0, 1, 1))]}
-        v_plan = {0: [(chunk_a0, ("V", 1, 0, 0)), (chunk_a0, ("V", 0, 0, QUART)), (chunk_a0, ("V", 1, 0, QUART))]}
+        v_plan = [(chunk_a0, ("V", 1, 0, 0)), (chunk_a0, ("V", 0, 0, QUART)), (chunk_a0, ("V", 1, 0, QUART))]
 
-        deferred = []
         for k in range(N_GROUPS):
             if k == 2:
                 late_loads()
             if k == 3:
                 c_tile(1, 1)
                 load_c(1, 1, 0, HALF)
-            gr = gpool.tile([P, QUART, NJ], BF16, tag="gr", name="gr", align_bytes=64)
-            gi = gpool.tile([P, QUART, NJ], BF16, tag="gi", name="gi", align_bytes=64)
-            g_il[k] = (gr, gi)
             for i in RB_MM_AT.get(k, ()):
                 rb_mm(i)
             pending = [fn(*args) for fn, args in plan.get(k, ())]
@@ -324,24 +323,30 @@ def tile_fourier_token_mixer_f4_kernel(
             pending += [fn(*args) for fn, args in plan2.get(k, ())]
             banks = [stage1(k, 0, s) for s in two]
             pa = [product(k, 0, s, banks[s]) for s in two]
-            while deferred:
-                g_im_sum(nc.vector, *deferred.pop())
-            for g_done in QUANT_G_AT.get(k, ()):
-                quant_g(g_done)
-            for n, (fn, args) in enumerate(v_plan.get(k, ())):
-                if n == 2:
-                    quant(*pending.pop(0))
-                pending.append(fn(*args))
+            if k == 0:
+                for n, (fn, args) in enumerate(v_plan):
+                    if n == 2:
+                        quant(*pending.pop(0))
+                    pending.append(fn(*args))
+                for item in pending:
+                    quant(*item)
+                pending = []
+            banks = [stage1(k, 1, s) for s in two]
+            pb = [product(k, 1, s, banks[s]) for s in two]
             for item in pending:
                 quant(*item)
-            banks = [stage1(k, 1, s) for s in two]
-            for s in two:
-                pb = product(k, 1, s, banks[s])
-                g_re_sum(nc.gpsimd, k, s, pa[s], pb)
-                if s == 1 and k in V_SUM_AFTER:
-                    deferred.append((k, s, pa[s], pb))
+            if k > 0:
+                quant_g(k - 1)
+            gr = gpool.tile([P, QUART, NJ], BF16, tag="gr", name="gr", align_bytes=64)
+            gi = gpool.tile([P, QUART, NJ], BF16, tag="gi", name="gi", align_bytes=64)
+            g_il[k] = (gr, gi)
+            for n in range(4):
+                s, part = n // 2, n % 2
+                eng = nc.vector if n in V_SUMS[k] else nc.gpsimd
+                if part == 0:
+                    g_re_sum(eng, k, s, pa[s], pb[s])
                 else:
-                    g_im_sum(nc.gpsimd, k, s, pa[s], pb)
+                    g_im_sum(eng, k, s, pa[s], pb[s])
 
         st = keep.tile([P, N_FT, 8], F32, name="st")
 
@@ -423,7 +428,6 @@ def tile_fourier_token_mixer_f4_kernel(
             nc.scalar.activation(out=u[:, es], in_=z[:, es], func=ACT.Identity, scale=stat(i, 5), bias=stat(i, 6))
             nc.gpsimd.tensor_tensor(out=z[:, es], in0=u[:, es], in1=gain_b[:, es], op=ALU.mult)
             nc.gpsimd.tensor_tensor(out=z[:, es], in0=z[:, es], in1=shift_b[:, es], op=ALU.add)
-            store(i, 0)
 
         def v_halves(i):
             return (1,) if i in G_TILES else (1, 0)
@@ -467,6 +471,8 @@ def tile_fourier_token_mixer_f4_kernel(
                     shift_v(i - 1, e)
                 if i - 1 in G_TILES:
                     normalize_g(i - 1)
+            if i - G_LAG in G_TILES:
+                store(i - G_LAG, 0)
             for g_done in QUANT_G_STEP.get(i, ()):
                 quant_g(g_done)
         i = N_FT - 1

@@ -25,15 +25,16 @@ ACT = mybir.ActivationFunctionType
 
 Z_SLOT = {0: "r3", 1: "r4", 2: "r2", 3: "r0", 4: "r1"}
 H_BANKS = 6
-V_SUMS = ((3,),) * 8
+V_SUMS = ((0,), (0, 1), (0,), (0, 1), (0,), (0, 1), (0,), (0,))
 QUANT_G_STEP = {1: (7,)}
-RB_MM_AT = {5: (0,), 6: (1,)}
-RB_OUT_AT = {5: (0,), 7: (1,)}
-RB_PRE = ((2, 4), (3, 6), (4, 2))
-G_TILES = (0, 1, 2, 3, 4)
-G_LAG = 3
-SPREAD_STEP = 4
-RB_STEP = {1: (5,), 2: (6,), 3: (7,)}
+RB_MM_AT = {5: (0,), 6: (1,), 7: (2,)}
+RB_OUT_AT = {5: (0,), 6: (1,), 7: (2,)}
+RB_PRE = ((3, 2), (4, 6), (5, 2), (6, 6))
+G_TILES = (0, 1, 2, 3, 4, 5)
+G_LAG = 2
+C_AT = {}
+SPREAD_STEP = 3
+RB_STEP = {1: (7,)}
 
 
 def tile_fourier_token_mixer_f4_kernel(
@@ -84,7 +85,7 @@ def tile_fourier_token_mixer_f4_kernel(
                 )
 
         def c_tile(q, h):
-            c_tiles[(q, h)] = cpool.tile([P, 2, NJ, HALF], BF16, tag="c", name="c")
+            c_tiles[(q, h)] = cpool.tile([P, 2, NJ, HALF], BF16, tag="c", name="c", align_bytes=64)
 
         x_raw = [raw_tile("r0")]
         a_raw = {(0, 0): raw_tile("r1"), (1, 0): raw_tile("r2")}
@@ -147,8 +148,8 @@ def tile_fourier_token_mixer_f4_kernel(
             )
             return il
 
-        def inter(eng, rows4):
-            il = il_tile()
+        def inter(eng, rows4, il=None):
+            il = il_tile() if il is None else il
             width = rows4.shape[2]
             copy_on(
                 eng,
@@ -162,8 +163,8 @@ def tile_fourier_token_mixer_f4_kernel(
                 out=dst[0][:, f : f + width].bitcast(FP8X4), scales=dst[1][:, f : f + width], in_=il[:, 0 : NJ * width]
             )
 
-        def inter_a0(eng, part, g, f):
-            return inter(eng, a_raw[(part, 0)][:, g, :, f : f + QUART])
+        def inter_a0(eng, part, g, f, il=None):
+            return inter(eng, a_raw[(part, 0)][:, g, :, f : f + QUART], il)
 
         def widen(q):
             wt = ring.tile([P, NJ, D], BF16, tag="r%d" % q, name="wr", align_bytes=64)
@@ -175,6 +176,10 @@ def tile_fourier_token_mixer_f4_kernel(
 
         def chunk_a0(eng, part, g, f):
             return inter_a0(eng, part, g, f), aq[(part, 0, g)], f, QUART
+
+        def chunk_last_a0():
+            il = gpool.tile([P, NJ * QUART], BF16, tag="gr", bufs=1, name="gr", align_bytes=64)
+            return inter_a0("S", 1, 1, QUART, il), aq[(1, 0, 1)], QUART, QUART
 
         def chunk_x1(g):
             return inter_x("S", 1, g), xq[(1, g)]
@@ -245,26 +250,32 @@ def tile_fourier_token_mixer_f4_kernel(
         def product(k, part, s, bank):
             fq, q = groups[k]
             h, f0 = fq // 2, (fq % 2) * QUART + s * P
-            dst = prod.tile([P, 2, P, NJ], F32, tag="p%d" % part, name="prod")
-            nc.vector.tensor_tensor(
-                out=dst[:],
-                in0=bank[:].rearrange("p t f -> p f t").unsqueeze(1).broadcast_to([P, 2, P, NJ]),
-                in1=c_tiles[(q, h)][:, :, :, f0 - 0 : f0 + P].rearrange("p c t f -> p c f t"),
-                op=ALU.mult,
-            )
+            dst = prod.tile([P, 2, 2, P, 2], F32, tag="p%d" % part, name="prod")
+            for pair in two:
+                ts = slice(2 * pair, 2 * pair + 2)
+                nc.vector.tensor_tensor(
+                    out=dst[:, pair],
+                    in0=bank[:, ts].rearrange("p t f -> p f t").unsqueeze(1).broadcast_to([P, 2, P, 2]),
+                    in1=c_tiles[(q, h)][:, :, ts, f0 : f0 + P].rearrange("p c t f -> p c f t"),
+                    op=ALU.mult,
+                )
             return dst
 
+        def of_c(dst, part):
+            return dst[:, :, part].rearrange("p a f b -> p f a b")
+
+        def out_g(k, part, s):
+            return g_il[k][part][:, s * P : (s + 1) * P].rearrange("p f (a b) -> p f a b", a=2)
+
         def g_re_sum(eng, k, s, pa, pb):
-            fs = slice(s * P, (s + 1) * P)
-            eng.tensor_tensor(out=g_il[k][0][:, fs], in0=pb[:, 1], in1=pa[:, 0], op=ALU.subtract)
+            eng.tensor_tensor(out=out_g(k, 0, s), in0=of_c(pb, 1), in1=of_c(pa, 0), op=ALU.subtract)
 
         def g_im_sum(eng, k, s, pa, pb):
-            fs = slice(s * P, (s + 1) * P)
-            eng.tensor_tensor(out=g_il[k][1][:, fs], in0=pa[:, 1], in1=pb[:, 0], op=ALU.add)
+            eng.tensor_tensor(out=out_g(k, 1, s), in0=of_c(pa, 1), in1=of_c(pb, 0), op=ALU.add)
 
         def quant_g(k):
             fq, q = groups[k]
-            for part in range(2):
+            for part in (1, 0):
                 dst = gq[(part, fq, q)]
                 nc.vector.quantize_mx(
                     out=dst[0][:].bitcast(FP8X4),
@@ -290,14 +301,12 @@ def tile_fourier_token_mixer_f4_kernel(
                 zt = ring.tile([P, 2, D], F32, tag=Z_SLOT[i], name="zu", align_bytes=64)
                 zu[i] = (zt[:, 0], zt[:, 1])
             else:
-                za = prod.tile([P, D], F32, tag="p0", name="za")
-                ua = prod.tile([P, D], F32, tag="p1", name="ua")
-                zu[i] = (za[:], ua[:])
+                zt = cpool.tile([P, 2, D], F32, tag="c", name="zc", align_bytes=64)
+                zu[i] = (zt[:, 0], zt[:, 1])
             for e in range(2):
                 nc.scalar.copy(out=zu[i][0][:, e * HALF : (e + 1) * HALF], in_=rb_banks[i][e][:])
 
         plan = {
-            0: [(chunk_a0, ("S", 1, 1, 0)), (chunk_a0, ("S", 0, 1, QUART)), (chunk_a0, ("S", 1, 1, QUART))],
             1: [(chunk_x1, (0,)), (chunk_x1, (1,))],
             2: [(chunk_a1, (0, 0))],
             3: [(chunk_a1, (0, 1)), (chunk_a1, (1, 0)), (chunk_a1, (1, 1))],
@@ -307,7 +316,7 @@ def tile_fourier_token_mixer_f4_kernel(
             7: [(chunk_w, (0, 1, 0))],
         }
         plan2 = {7: [(chunk_w, (0, 1, 1))]}
-        v_plan = [(chunk_a0, ("V", 1, 0, 0)), (chunk_a0, ("V", 0, 0, QUART)), (chunk_a0, ("V", 1, 0, QUART))]
+        s_first = [(chunk_a0, ("S", 0, 0, QUART)), (chunk_a0, ("S", 0, 1, QUART)), (chunk_a0, ("S", 1, 0, QUART)), (chunk_last_a0, ())]
 
         for k in range(N_GROUPS):
             if k == 2:
@@ -321,32 +330,31 @@ def tile_fourier_token_mixer_f4_kernel(
             for i in RB_OUT_AT.get(k, ()):
                 rb_out(i)
             pending += [fn(*args) for fn, args in plan2.get(k, ())]
+            if k == 0:
+                first = [chunk_a0("S", 1, 1, 0)]
+                pending = [fn(*args) for fn, args in s_first]
             banks = [stage1(k, 0, s) for s in two]
             pa = [product(k, 0, s, banks[s]) for s in two]
             if k == 0:
-                for n, (fn, args) in enumerate(v_plan):
-                    if n == 2:
-                        quant(*pending.pop(0))
-                    pending.append(fn(*args))
-                for item in pending:
+                first.append(chunk_a0("V", 1, 0, 0))
+                for item in first:
                     quant(*item)
-                pending = []
             banks = [stage1(k, 1, s) for s in two]
             pb = [product(k, 1, s, banks[s]) for s in two]
+            gr = gpool.tile([P, QUART, NJ], BF16, tag="gr", bufs=1, name="gr", align_bytes=64)
+            gi = gpool.tile([P, QUART, NJ], BF16, tag="gi", bufs=2, name="gi", align_bytes=64)
+            g_il[k] = (gr, gi)
             for item in pending:
                 quant(*item)
+            for s in V_SUMS[k]:
+                g_im_sum(nc.vector, k, s, pa[s], pb[s])
             if k > 0:
                 quant_g(k - 1)
-            gr = gpool.tile([P, QUART, NJ], BF16, tag="gr", name="gr", align_bytes=64)
-            gi = gpool.tile([P, QUART, NJ], BF16, tag="gi", name="gi", align_bytes=64)
-            g_il[k] = (gr, gi)
-            for n in range(4):
-                s, part = n // 2, n % 2
-                eng = nc.vector if n in V_SUMS[k] else nc.gpsimd
-                if part == 0:
-                    g_re_sum(eng, k, s, pa[s], pb[s])
-                else:
-                    g_im_sum(eng, k, s, pa[s], pb[s])
+            for s in two:
+                g_re_sum(nc.gpsimd, k, s, pa[s], pb[s])
+            for s in two:
+                if s not in V_SUMS[k]:
+                    g_im_sum(nc.gpsimd, k, s, pa[s], pb[s])
 
         st = keep.tile([P, N_FT, 8], F32, name="st")
 

from contextlib import ExitStack

import concourse.mybir as mybir
from concourse.masks import make_identity

T = 1024
D = 1024
FLOPS = 8 * D * T * T

P = 128
NJ = 4
HALF = 512
QUART = 256
N_GROUPS = 8
N_FT = 8

F32 = mybir.dt.float32
BF16 = mybir.dt.bfloat16
U32 = mybir.dt.uint32
U8 = mybir.dt.uint8
FP8 = mybir.dt.float8_e4m3fn
FP8X4 = mybir.dt.float8_e4m3fn_x4
ALU = mybir.AluOpType
ACT = mybir.ActivationFunctionType

Z_SLOT = {0: "r3", 1: "r4", 2: "r2", 3: "r0", 4: "r1"}
H_BANKS = 6
V_SUMS = ((0,), (0, 1), (0,), (0, 1), (0,), (0, 1), (0,), (0,))
QUANT_G_STEP = {1: (7,)}
RB_MM_AT = {5: (0,), 6: (1,), 7: (2,)}
RB_OUT_AT = {5: (0,), 6: (1,), 7: (2,)}
RB_PRE = ((3, 2), (4, 6), (5, 2), (6, 6))
G_TILES = (0, 1, 2, 3, 4, 5)
G_LAG = 2
C_AT = {}
SPREAD_STEP = 3
RB_STEP = {1: (7,)}


def tile_fourier_token_mixer_f4_kernel(
    tc, x, a_re, a_im, c_re, c_im, w_re_bytes, w_re_scale, w_im, bias, resid, gain, shift, out
):
    nc = tc.nc
    with ExitStack() as ctx:
        keep = ctx.enter_context(tc.tile_pool(name="keep", bufs=1))
        ring = ctx.enter_context(tc.tile_pool(name="ring", bufs=1))
        cpool = ctx.enter_context(tc.tile_pool(name="cpool", bufs=3))
        ilpool = ctx.enter_context(tc.tile_pool(name="ilpool", bufs=7))
        gpool = ctx.enter_context(tc.tile_pool(name="gpool", bufs=1))
        prod = ctx.enter_context(tc.tile_pool(name="prod", bufs=4))
        psum = ctx.enter_context(tc.psum_pool(name="psum", bufs=1))
        ctx.enter_context(tc.manual_schedule())

        ident = keep.tile([P, P], BF16, name="ident")
        ones = keep.tile([P, P], BF16, name="ones")
        rows = keep.tile([P, 3, D], BF16, name="rows")
        tiny = keep.tile([P, 1], F32, name="tiny")
        nc.gpsimd.memset(tiny[:], 1.0)
        nc.scalar.activation(out=tiny[:], in_=tiny[:], func=ACT.Abs_reciprocal_sqrt)
        make_identity(nc, ident[:])
        nc.gpsimd.memset(ones[:], 1.0)
        nc.gpsimd.memset(rows[:], 0.0)

        xv = x.rearrange("(g p j) d -> p g j d", g=2, j=NJ)
        av = (a_re.rearrange("(g p j) f -> p g j f", g=2, j=NJ), a_im.rearrange("(g p j) f -> p g j f", g=2, j=NJ))
        cv = (c_re.rearrange("(q p t) f -> p q t f", q=2, t=NJ), c_im.rearrange("(q p t) f -> p q t f", q=2, t=NJ))
        wbv = w_re_bytes.rearrange("(q p j) e -> p q j e", q=2, j=NJ)
        wiv = w_im.rearrange("(q p j) e -> p q j e", q=2, j=NJ)
        scv = w_re_scale.rearrange("(q p j) o -> p q (j o)", q=2, j=NJ)
        rv = resid.rearrange("(i p) e -> p i e", p=P)

        def raw_tile(tag):
            return ring.tile([P, 2, NJ, HALF], BF16, tag=tag, name="raw", align_bytes=64)

        def load(raw, view, g, src, dst, width):
            nc.sync.dma_start(out=raw[:, g, :, dst : dst + width], in_=view[:, g, :, src : src + width])

        c_tiles = {}

        def load_c(q, h, f, width):
            for part in range(2):
                nc.sync.dma_start(
                    out=c_tiles[(q, h)][:, part, :, f : f + width],
                    in_=cv[part][:, q, :, h * HALF + f : h * HALF + f + width],
                )

        def c_tile(q, h):
            c_tiles[(q, h)] = cpool.tile([P, 2, NJ, HALF], BF16, tag="c", name="c", align_bytes=64)

        x_raw = [raw_tile("r0")]
        a_raw = {(0, 0): raw_tile("r1"), (1, 0): raw_tile("r2")}
        for g in range(2):
            load(x_raw[0], xv, g, 0, 0, HALF)
        c_tile(0, 0)
        for f in (0, QUART):
            for g in range(2):
                load(a_raw[(0, 0)], av[0], g, f, f, QUART)
            if f == 0:
                load_c(0, 0, f, QUART)
            for g in range(2):
                load(a_raw[(1, 0)], av[1], g, f, f, QUART)
            if f > 0:
                load_c(0, 0, f, QUART)
        x_raw.append(raw_tile("r3"))
        for g in range(2):
            load(x_raw[1], xv, g, HALF, 0, HALF)
        c_tile(1, 0)
        load_c(1, 0, 0, HALF)
        a_raw[(0, 1)] = raw_tile("r4")
        for g in range(2):
            load(a_raw[(0, 1)], av[0], g, HALF, 0, HALF)

        wscale = keep.tile([P, 2, NJ], F32, name="wscale")
        wbytes = keep.tile([P, 2, NJ, D], U8, name="wbytes")
        res = keep.tile([P, N_FT, D], BF16, name="res")
        gain_b = keep.tile([P, D], BF16, name="gain_b")
        shift_b = keep.tile([P, D], BF16, name="shift_b")

        def codes_tile(name, width):
            return (
                keep.tile([P, width], U32, name=name + "_c", align_bytes=64),
                keep.tile([P, width], U8, name=name + "_s", align_bytes=64),
            )

        two = range(2)
        xq = {(q, g): codes_tile("xq%d%d" % (q, g), HALF) for q in two for g in two}
        aq = {(part, h, g): codes_tile("aq%d%d%d" % (part, h, g), HALF) for part in two for h in two for g in two}
        wq = {(part, q, e): codes_tile("wq%d%d%d" % (part, q, e), HALF) for part in two for q in two for e in two}
        gq = {
            (part, fq, q): codes_tile("gq%d%d%d" % (part, fq, q), QUART) for part in two for fq in range(4) for q in two
        }

        def il_tile():
            return ilpool.tile([P, NJ * HALF], BF16, tag="il", name="il", align_bytes=64)

        def copy_on(eng, o, i):
            if eng == "V":
                nc.vector.tensor_copy(out=o, in_=i)
            else:
                nc.scalar.copy(out=o, in_=i)

        def inter_x(eng, q, g):
            il = il_tile()
            copy_on(
                eng,
                il[:].rearrange("p (t m j) -> p m t j", t=NJ, j=NJ),
                x_raw[q][:, g].rearrange("p j (m t) -> p m t j", t=NJ),
            )
            return il

        def inter(eng, rows4, il=None):
            il = il_tile() if il is None else il
            width = rows4.shape[2]
            copy_on(
                eng,
                il[:, 0 : NJ * width].rearrange("p (c i j) -> p c j i", i=4, j=NJ),
                rows4.rearrange("p j (c i) -> p c j i", i=4),
            )
            return il

        def quant(il, dst, f=0, width=HALF):
            nc.vector.quantize_mx(
                out=dst[0][:, f : f + width].bitcast(FP8X4), scales=dst[1][:, f : f + width], in_=il[:, 0 : NJ * width]
            )

        def inter_a0(eng, part, g, f, il=None):
            return inter(eng, a_raw[(part, 0)][:, g, :, f : f + QUART], il)

        def widen(q):
            wt = ring.tile([P, NJ, D], BF16, tag="r%d" % q, name="wr", align_bytes=64)
            for j in range(NJ):
                nc.scalar.activation(
                    out=wt[:, j], in_=wbytes[:, q, j].bitcast(FP8), func=ACT.Copy, scale=wscale[:, q, j : j + 1]
                )
            w_raw[(0, q)] = wt

        def chunk_a0(eng, part, g, f):
            return inter_a0(eng, part, g, f), aq[(part, 0, g)], f, QUART

        def chunk_last_a0():
            il = gpool.tile([P, NJ * QUART], BF16, tag="gr", bufs=1, name="gr", align_bytes=64)
            return inter_a0("S", 1, 1, QUART, il), aq[(1, 0, 1)], QUART, QUART

        def chunk_x1(g):
            return inter_x("S", 1, g), xq[(1, g)]

        def chunk_a1(part, g):
            return inter("S", a_raw[(part, 1)][:, g]), aq[(part, 1, g)]

        w_raw = {}

        def chunk_w(part, q, e):
            if part == 0 and e == 0:
                widen(q)
            return inter("S", w_raw[(part, q)][:, :, e * HALF : (e + 1) * HALF]), wq[(part, q, e)]

        xi0 = inter_x("V", 0, 0)
        xi1 = inter_x("V", 0, 1)
        re0 = inter_a0("S", 0, 0, 0)
        re1 = inter_a0("S", 0, 1, 0)
        quant(xi0, xq[(0, 0)])
        quant(xi1, xq[(0, 1)])
        quant(re0, aq[(0, 0, 0)], 0, QUART)
        quant(re1, aq[(0, 0, 1)], 0, QUART)
        a_raw[(1, 1)] = raw_tile("r0")
        for g in range(2):
            load(a_raw[(1, 1)], av[1], g, HALF, 0, HALF)
        nc.sync.dma_start(out=wscale[:], in_=scv)
        for q in range(2):
            wt = ring.tile([P, NJ, D], BF16, tag="r%d" % (1 + q), name="wi", align_bytes=64)
            w_raw[(1, q)] = wt
        c_tile(0, 1)
        load_c(0, 1, 0, HALF)

        def late_loads():
            for q in range(2):
                nc.sync.dma_start(out=w_raw[(1, q)][:], in_=wiv[:, q])
            for r, vec in enumerate((bias, gain, shift)):
                nc.sync.dma_start(out=rows[0:1, r, :], in_=vec.rearrange("(o e) -> o e", o=1))
            nc.sync.dma_start(out=res[:, 0:4], in_=rv[:, 0:4])
            for q in range(2):
                nc.sync.dma_start(out=wbytes[:, q], in_=wbv[:, q])
            nc.sync.dma_start(out=res[:, 4:8], in_=rv[:, 4:8])
            nc.sync.dma_start(out=gain_b[:], in_=gain.partition_broadcast(P))
            nc.sync.dma_start(out=shift_b[:], in_=shift.partition_broadcast(P))

        groups = [(0, 0), (1, 0), (0, 1), (1, 1), (2, 0), (3, 0), (2, 1), (3, 1)]
        g_il = {}

        def bank_tile(b, shape, name):
            return psum.tile(shape, F32, tag="b%d" % b, name=name)

        def stage1(k, part, s):
            fq, q = groups[k]
            h, f0 = fq // 2, (fq % 2) * QUART + s * P
            bank = bank_tile((4 * k + 2 * part + s) % H_BANKS, [P, NJ, P], "h")
            for t in range(NJ):
                for g in range(2):
                    nc.tensor.matmul_mx(
                        out=bank[:, t],
                        lhsT=xq[(q, g)][0][:, t * P : (t + 1) * P].bitcast(FP8X4),
                        lhsT_scale=xq[(q, g)][1][:, t * P : (t + 1) * P],
                        rhs=aq[(part, h, g)][0][:, f0 : f0 + P].bitcast(FP8X4),
                        rhs_scale=aq[(part, h, g)][1][:, f0 : f0 + P],
                        start=(g == 0),
                        stop=(g == 1),
                    )
            return bank

        def product(k, part, s, bank):
            fq, q = groups[k]
            h, f0 = fq // 2, (fq % 2) * QUART + s * P
            dst = prod.tile([P, 2, 2, P, 2], F32, tag="p%d" % part, name="prod")
            for pair in two:
                ts = slice(2 * pair, 2 * pair + 2)
                nc.vector.tensor_tensor(
                    out=dst[:, pair],
                    in0=bank[:, ts].rearrange("p t f -> p f t").unsqueeze(1).broadcast_to([P, 2, P, 2]),
                    in1=c_tiles[(q, h)][:, :, ts, f0 : f0 + P].rearrange("p c t f -> p c f t"),
                    op=ALU.mult,
                )
            return dst

        def of_c(dst, part):
            return dst[:, :, part].rearrange("p a f b -> p f a b")

        def out_g(k, part, s):
            return g_il[k][part][:, s * P : (s + 1) * P].rearrange("p f (a b) -> p f a b", a=2)

        def g_re_sum(eng, k, s, pa, pb):
            eng.tensor_tensor(out=out_g(k, 0, s), in0=of_c(pb, 1), in1=of_c(pa, 0), op=ALU.subtract)

        def g_im_sum(eng, k, s, pa, pb):
            eng.tensor_tensor(out=out_g(k, 1, s), in0=of_c(pa, 1), in1=of_c(pb, 0), op=ALU.add)

        def quant_g(k):
            fq, q = groups[k]
            for part in (1, 0):
                dst = gq[(part, fq, q)]
                nc.vector.quantize_mx(
                    out=dst[0][:].bitcast(FP8X4),
                    scales=dst[1][:],
                    in_=g_il[k][part][:].rearrange("p f t -> p (f t)"),
                )

        zu = {}

        rb_banks = {}

        def rb_mm(i, b=6):
            rb_banks[i] = []
            for e in range(2):
                es = slice(e * HALF, (e + 1) * HALF)
                bank = bank_tile(b + e, [P, HALF], "rb")
                nc.tensor.matmul(out=bank[:], lhsT=ident[:], rhs=res[:, i, es], start=True, stop=False)
                nc.tensor.matmul(out=bank[:], lhsT=ones[:], rhs=rows[:, 0, es], start=False, stop=True)
                rb_banks[i].append(bank)

        def rb_out(i):
            if i in Z_SLOT:
                zt = ring.tile([P, 2, D], F32, tag=Z_SLOT[i], name="zu", align_bytes=64)
                zu[i] = (zt[:, 0], zt[:, 1])
            else:
                zt = cpool.tile([P, 2, D], F32, tag="c", name="zc", align_bytes=64)
                zu[i] = (zt[:, 0], zt[:, 1])
            for e in range(2):
                nc.scalar.copy(out=zu[i][0][:, e * HALF : (e + 1) * HALF], in_=rb_banks[i][e][:])

        plan = {
            1: [(chunk_x1, (0,)), (chunk_x1, (1,))],
            2: [(chunk_a1, (0, 0))],
            3: [(chunk_a1, (0, 1)), (chunk_a1, (1, 0)), (chunk_a1, (1, 1))],
            4: [(chunk_w, (1, 0, 0))],
            5: [(chunk_w, (1, 0, 1)), (chunk_w, (1, 1, 0)), (chunk_w, (1, 1, 1))],
            6: [(chunk_w, (0, 0, 0)), (chunk_w, (0, 0, 1))],
            7: [(chunk_w, (0, 1, 0))],
        }
        plan2 = {7: [(chunk_w, (0, 1, 1))]}
        s_first = [(chunk_a0, ("S", 0, 0, QUART)), (chunk_a0, ("S", 0, 1, QUART)), (chunk_a0, ("S", 1, 0, QUART)), (chunk_last_a0, ())]

        for k in range(N_GROUPS):
            if k == 2:
                late_loads()
            if k == 3:
                c_tile(1, 1)
                load_c(1, 1, 0, HALF)
            for i in RB_MM_AT.get(k, ()):
                rb_mm(i)
            pending = [fn(*args) for fn, args in plan.get(k, ())]
            for i in RB_OUT_AT.get(k, ()):
                rb_out(i)
            pending += [fn(*args) for fn, args in plan2.get(k, ())]
            if k == 0:
                first = [chunk_a0("S", 1, 1, 0)]
                pending = [fn(*args) for fn, args in s_first]
            banks = [stage1(k, 0, s) for s in two]
            pa = [product(k, 0, s, banks[s]) for s in two]
            if k == 0:
                first.append(chunk_a0("V", 1, 0, 0))
                for item in first:
                    quant(*item)
            banks = [stage1(k, 1, s) for s in two]
            pb = [product(k, 1, s, banks[s]) for s in two]
            gr = gpool.tile([P, QUART, NJ], BF16, tag="gr", bufs=1, name="gr", align_bytes=64)
            gi = gpool.tile([P, QUART, NJ], BF16, tag="gi", bufs=2, name="gi", align_bytes=64)
            g_il[k] = (gr, gi)
            for item in pending:
                quant(*item)
            for s in V_SUMS[k]:
                g_im_sum(nc.vector, k, s, pa[s], pb[s])
            if k > 0:
                quant_g(k - 1)
            for s in two:
                g_re_sum(nc.gpsimd, k, s, pa[s], pb[s])
            for s in two:
                if s not in V_SUMS[k]:
                    g_im_sum(nc.gpsimd, k, s, pa[s], pb[s])

        st = keep.tile([P, N_FT, 8], F32, name="st")

        def stat(i, j):
            return st[:, i, j : j + 1]

        def stage2(i):
            fq, f0 = i // 2, (i % 2) * P
            banks = []
            for e in range(2):
                bank = bank_tile(4 + 2 * (i % 2) + e, [P, HALF], "y")
                n = 0
                for q in range(2):
                    for part in (1, 0):
                        nc.tensor.matmul_mx(
                            out=bank[:],
                            lhsT=gq[(part, fq, q)][0][:, f0 : f0 + P].bitcast(FP8X4),
                            lhsT_scale=gq[(part, fq, q)][1][:, f0 : f0 + P],
                            rhs=wq[(part, q, e)][0][:].bitcast(FP8X4),
                            rhs_scale=wq[(part, q, e)][1][:],
                            start=(n == 0),
                            stop=(n == 3),
                        )
                        n += 1
                banks.append(bank)
            return banks

        def finish_z(i, e, banks):
            zs = zu[i][0][:, e * HALF : (e + 1) * HALF]
            nc.vector.scalar_tensor_tensor(
                out=zs, in0=banks[e][:], scalar=-1.0, in1=zs, op0=ALU.mult, op1=ALU.add, accum_out=stat(i, e)
            )

        def neg_mean(i):
            nc.vector.tensor_scalar(
                out=stat(i, 2), in0=stat(i, 0), scalar1=stat(i, 1), scalar2=-1.0 / D, op0=ALU.add, op1=ALU.mult
            )

        def spread_of_z(i):
            z, u = zu[i]
            nc.scalar.activation(out=u, in_=z, func=ACT.Square, bias=stat(i, 2), accum_out=stat(i, 3))
            nc.scalar.activation(out=stat(i, 5), in_=stat(i, 3), func=ACT.Abs_reciprocal_sqrt, scale=1.0 / D)

        ov = out.rearrange("(i p) e -> i p e", p=P)

        def store(i, e):
            es = slice(e * HALF, (e + 1) * HALF)
            nc.sync.dma_start(out=ov[i][:, es], in_=zu[i][0][:, es])

        def scale_v(i, e):
            z, u = zu[i]
            es = slice(e * HALF, (e + 1) * HALF)
            nc.vector.scalar_tensor_tensor(
                out=u[:, es],
                in0=z[:, es],
                scalar=stat(i, 2),
                in1=spread[(1, e)][:],
                op0=ALU.add,
                op1=ALU.mult,
            )

        def shift_v(i, e):
            z, u = zu[i]
            es = slice(e * HALF, (e + 1) * HALF)
            nc.vector.scalar_tensor_tensor(
                out=z[:, es],
                in0=u[:, es],
                scalar=stat(i, 5),
                in1=spread[(2, e)][:],
                op0=ALU.mult,
                op1=ALU.add,
            )
            store(i, e)

        def normalize_g(i):
            z, u = zu[i]
            es = slice(0, HALF)
            nc.scalar.activation(out=stat(i, 6), in_=stat(i, 2), func=ACT.Copy, scale=stat(i, 5))
            nc.scalar.activation(out=u[:, es], in_=z[:, es], func=ACT.Identity, scale=stat(i, 5), bias=stat(i, 6))
            nc.gpsimd.tensor_tensor(out=z[:, es], in0=u[:, es], in1=gain_b[:, es], op=ALU.mult)
            nc.gpsimd.tensor_tensor(out=z[:, es], in0=z[:, es], in1=shift_b[:, es], op=ALU.add)

        def v_halves(i):
            return (1,) if i in G_TILES else (1, 0)

        y_banks = {}
        for i, b in RB_PRE:
            rb_mm(i, b)
            rb_out(i)
        for i in range(2):
            y_banks[i] = stage2(i)
        spread = {}

        def spread_mm(r, e, b):
            bank = bank_tile(b, [P, HALF], "spread")
            nc.tensor.matmul(
                out=bank[:], lhsT=ones[:], rhs=rows[:, r, e * HALF : (e + 1) * HALF], start=True, stop=True
            )
            spread[(r, e)] = bank

        for r in (1, 2):
            spread_mm(r, 1, r - 1)
        for i in range(N_FT):
            finish_z(i, 0, y_banks[i])
            finish_z(i, 1, y_banks[i])
            for j in RB_STEP.get(i, ()):
                rb_mm(j, 2)
            if i + 2 < N_FT:
                y_banks[i + 2] = stage2(i + 2)
            if i >= 1:
                for e in v_halves(i - 1):
                    scale_v(i - 1, e)
            neg_mean(i)
            spread_of_z(i)
            for j in RB_STEP.get(i, ()):
                rb_out(j)
            if i == SPREAD_STEP:
                for r in (1, 2):
                    spread_mm(r, 0, r + 1)
            if i >= 1:
                for e in v_halves(i - 1):
                    shift_v(i - 1, e)
                if i - 1 in G_TILES:
                    normalize_g(i - 1)
            if i - G_LAG in G_TILES:
                store(i - G_LAG, 0)
            for g_done in QUANT_G_STEP.get(i, ()):
                quant_g(g_done)
        i = N_FT - 1
        scale_v(i, 1)
        scale_v(i, 0)
        shift_v(i, 1)
        shift_v(i, 0)
